import numpy as np
import ml_dtypes


def mxq(x, axis, fmt="e4m3"):
    dtype, down = {"e4m3": (ml_dtypes.float8_e4m3fn, 7), "e5m2": (ml_dtypes.float8_e5m2, 14)}[fmt]
    v = np.moveaxis(np.asarray(x, np.float32).astype(ml_dtypes.bfloat16).astype(np.float64), axis, -1)
    blocks = v.reshape(v.shape[:-1] + (-1, 32))
    amax = np.abs(blocks).max(-1, keepdims=True)
    byte = np.maximum(np.where(amax > 0, np.frexp(amax)[1] - 1 + 127, 0) - down, 1)
    scale = np.exp2(byte - 127.0)
    codes = (blocks / scale).astype(np.float32).astype(dtype).astype(np.float64)
    return np.moveaxis((codes * scale).reshape(v.shape), -1, axis)


WIDE = False


def mx_kscale(k):
    if not WIDE:
        return np.ones(k)
    levels = np.array([10, -10, 5, -5, 0])
    if k % 512:
        return np.exp2(np.random.permutation(np.resize(levels, k // 32))).repeat(32)
    a = np.empty((k // 512, 16))
    for p in range(k // 512):
        a[p, :8] = np.random.permutation(np.resize(levels, 8))
        for g in range(8):
            far = levels[np.abs(levels - a[p, g]) >= 10]
            a[p, g + 8] = far[np.random.randint(len(far))]
    return np.exp2(a.ravel()).repeat(32)


def f64(x):
    return np.asarray(x).astype(np.float64)


def striped(idx):
    return np.tile(idx.reshape(-1, 16).T, (8, 1)).astype(np.uint16)


def unstriped(offs):
    return offs[:16].T.reshape(-1).astype(np.int64)


E2M1 = np.array([0.0, 0.5, 1.0, 1.5, 2.0, 3.0, 4.0, 6.0, -0.0, -0.5, -1.0, -1.5, -2.0, -3.0, -4.0, -6.0])


def pack_weight(w, fmt):
    k, n = w.shape
    w = f64(np.asarray(w, np.float32).astype(ml_dtypes.bfloat16)).reshape(k // 32, 32, n)
    amax = np.abs(w).max(1)
    if fmt == "e4m3":
        byte = np.frexp(amax)[1] - 1 + 127 - 7
    else:
        mant, ex = np.frexp(amax / 6.0)
        byte = np.where(mant > 0.5, ex, ex - 1) + 127
    byte = np.clip(np.where(amax > 0, byte, 1), 1, 254)
    scaled = (w * np.exp2(127.0 - byte)[:, None, :]).reshape(k, n).astype(np.float32)
    by_word = np.ascontiguousarray(scaled.reshape(k // 512, 128, 4, n).transpose(0, 1, 3, 2))
    if fmt == "e4m3":
        words = by_word.astype(ml_dtypes.float8_e4m3fn).view(np.uint8)
    else:
        c = by_word.astype(ml_dtypes.float4_e2m1fn).view(np.uint8) & 0xF
        words = (c[..., 0::2] | (c[..., 1::2] << 4)).reshape(k // 512, 128, 2 * n)
    return np.ascontiguousarray(words), np.ascontiguousarray(byte.astype(np.uint8).reshape(k // 512, 16, n))


def unpack_weight(words, scales, fmt):
    g, _, n = scales.shape
    words = np.ascontiguousarray(words).reshape(g, 128, n, -1)
    if fmt == "e4m3":
        vals = words.view(ml_dtypes.float8_e4m3fn).astype(np.float64)
    else:
        nib = np.empty((g, 128, n, 4), np.uint8)
        nib[..., 0::2] = words & 0xF
        nib[..., 1::2] = words >> 4
        vals = E2M1[nib]
    vals = vals * np.repeat(np.exp2(scales.astype(np.float64) - 127.0), 8, axis=1)[..., None]
    return vals.transpose(0, 1, 3, 2).reshape(g * 512, n)


def gelu(v):
    return 0.5 * v * (1.0 + np.tanh(np.sqrt(2.0 / np.pi) * (v + 0.044715 * v**3)))


def striped8(idx):
    return np.concatenate([v.reshape(-1, 16).T for v in idx]).astype(np.uint16)


def unstriped8(offs):
    return np.stack([offs[16 * g:16 * g + 16].T.reshape(-1) for g in range(8)]).astype(np.int64)


def put_heads(h, wgs, idx8, t2):
    r = np.arange(h.shape[0])
    page = np.zeros((h.shape[0], t2))
    page[r[:, None], idx8[r % 512 // 64]] = wgs[r // 4 % 128] * h
    return page


def bf(x):
    return np.asarray(x, np.float32).astype(ml_dtypes.bfloat16)


def planes(Y):
    n, m = Y.shape
    b = f64(bf(Y)).reshape(n // 32, 32, m)
    amax = np.abs(b).max(1)
    byte = np.clip(np.where(amax > 0, np.frexp(amax)[1] - 1 + 127 - 7, 1), 1, 254)
    codes = (b * np.exp2(127.0 - byte)[:, None, :]).reshape(n, m).astype(np.float32).astype(ml_dtypes.float8_e4m3fn).view(np.uint8)
    words = codes.reshape(n // 512, 128, 4, m).transpose(0, 1, 3, 2)
    return np.ascontiguousarray(words), np.ascontiguousarray(byte.astype(np.uint8).reshape(n // 512, 16, m))


K, T, S, T2, H, N = 1024, 4096, 1024, 2048, 1024, 512


def setup_inputs():
    n = np.random.standard_normal
    s = mx_kscale(K)[:, None]
    u = mx_kscale(H)[:, None]
    tab_words, tab_scales = pack_weight(n((K, T)) * s, "e4m3")
    w1_words, w1_scales = pack_weight(n((K, H)) / np.sqrt(K) / s, "e2m1")
    share = np.random.uniform(0.3, 0.8, H)
    old = n((H, T2))
    size = np.exp(0.8 * n(N))
    w2 = n((H, N)) / np.sqrt(H) * size[None, :] / u
    floor = -size * np.random.uniform(0.4, 1.0, N)
    return {
        "tab_words": tab_words, "tab_scales": tab_scales,
        "offs": striped(np.random.permutation(T)[:S]),
        "w1_words": w1_words, "w1_scales": w1_scales,
        "offs2": striped8(np.stack([np.random.permutation(T2)[:S] for _ in range(8)])),
        "wgs": np.repeat(np.random.uniform(0.5, 2.0, (8, S)), 16, axis=0).astype(np.float32),
        "rate": (share * u[:, 0]).astype(np.float32),
        "kept": ((1.0 - share)[:, None] * old * u).astype(np.float32),
        "w2": w2.astype(np.float32),
        "floor": floor.astype(np.float32),
    }


def reference(tab_words, tab_scales, offs, w1_words, w1_scales, offs2, wgs, rate, kept, w2, floor):
    v = unpack_weight(tab_words, tab_scales, "e4m3")[:, unstriped(offs)]
    w1 = unpack_weight(w1_words, w1_scales, "e2m1")
    a = w1.T @ v
    h = np.sqrt(1.0 + np.square(a))
    page = put_heads(h, f64(wgs), unstriped8(offs2), T2)
    z = f64(rate)[:, None] * page + f64(kept)
    y = mxq(f64(w2), 0, "e4m3").T @ mxq(z, 0, "e4m3")
    y = np.maximum(y, f64(floor)[:, None])
    words, scales = planes(y)
    return y, words, scales

@@ -1,0 +1,347 @@
+from contextlib import ExitStack
+
+import concourse.mybir as mybir
+from concourse.masks import make_identity
+
+K, T, S, T2, H, N = 1024, 4096, 1024, 2048, 1024, 512
+FLOPS = 2 * K * H * S + 2 * H * N * T2
+
+F32 = mybir.dt.float32
+BF16 = mybir.dt.bfloat16
+I32 = mybir.dt.int32
+U32 = mybir.dt.uint32
+U16 = mybir.dt.uint16
+U8 = mybir.dt.uint8
+FP8X4 = mybir.dt.float8_e4m3fn_x4
+FP4X4 = mybir.dt.float4_e2m1fn_x4
+ACT = mybir.ActivationFunctionType
+ALU = mybir.AluOpType
+
+P = 128
+BANK = 512
+PASSES = 2
+TILES = 8
+PAGES = 4
+BLOCKS = T2 // P
+CHUNKS = T2 // BANK
+AL = 64
+
+
+def tile_list_berth_page_nowcast_kernel(
+    tc, tab_words, tab_scales, offs, w1_words, w1_scales, offs2, wgs, rate, kept, w2, floor, out_0, out_1, out_2
+):
+    nc = tc.nc
+    with ExitStack() as ctx:
+        held = ctx.enter_context(tc.tile_pool(name="held", bufs=1))
+        ring = ctx.enter_context(tc.tile_pool(name="ring", bufs=1))
+        psum = ctx.enter_context(tc.psum_pool(name="psum", bufs=1))
+
+        def sb(name, cols, dtype, tag=None, bufs=1):
+            if tag is None:
+                return held.tile([P, cols], dtype, name=name, align_bytes=AL)
+            return ring.tile([P, cols], dtype, name=name, tag=tag, bufs=bufs, align_bytes=AL)
+
+        def bank(i, name):
+            return psum.tile([P, BANK], F32, name=name, tag="bank%d" % i)
+
+        list1 = held.tile([P, S // 16], U16, name="list1")
+        list2 = held.tile([P, S // 16], U16, name="list2")
+        rate_sb = sb("rate_sb", TILES, F32)
+        floor_sb = sb("floor_sb", 4, F32)
+        one = sb("one", 1, F32)
+        warm = sb("warm", 1, F32)
+        ident = sb("ident", P, F32)
+
+        tab_sc = sb("tab_sc", PASSES * T, U8, tag="w2_raw")
+        seed = sb("seed", 1, F32, tag="big")
+        wgs_sb = sb("wgs_sb", S, F32, tag="sq", bufs=2)
+        w1_raw = sb("w1_raw", PASSES * 2 * H, U8, tag="page0")
+        w1_sc_raw = sb("w1_sc_raw", PASSES * H, U8, tag="page1")
+
+        nc.vector.memset(tab_sc[:].bitcast(I32), 0)
+        nc.vector.memset(seed[:], 1.0)
+        nc.vector.tensor_copy(one[:], seed[:])
+        nc.vector.memset(w1_sc_raw[:].bitcast(I32), 0)
+
+        nc.sync.dma_start(list1[:], offs)
+        nc.sync.dma_start(
+            w1_raw[:].bitcast(I32).rearrange("p (a c) -> p a c", a=PASSES),
+            w1_words.bitcast(I32).rearrange("a p c -> p a c"),
+        )
+        for q in range(4):
+            nc.sync.dma_start(
+                tab_sc[32 * q : 32 * q + 4, :].bitcast(I32).rearrange("r (a c) -> r a c", a=PASSES),
+                tab_scales[:, 4 * q : 4 * q + 4, :].bitcast(I32).rearrange("a r c -> r a c"),
+            )
+        for q in range(4):
+            nc.scalar.dma_start(
+                w1_sc_raw[32 * q : 32 * q + 4, :].bitcast(I32).rearrange("r (a c) -> r a c", a=PASSES),
+                w1_scales[:, 4 * q : 4 * q + 4, :].bitcast(I32).rearrange("a r c -> r a c"),
+            )
+        nc.sync.dma_start(wgs_sb[:], wgs)
+        tab_sb = sb("tab_sb", PASSES * T, I32, tag="big")
+        tab = [tab_sb[:, a * T : (a + 1) * T] for a in range(PASSES)]
+        for a in range(PASSES):
+            nc.sync.dma_start(tab[a], tab_words[a].rearrange("p c i -> p (c i)").bitcast(I32))
+        nc.gpsimd.dma_start(
+            rate_sb[:].rearrange("p (b t) -> p b t", b=PASSES), rate.rearrange("(b p t) -> p b t", b=PASSES, t=4)
+        )
+
+        make_identity(nc, ident[:])
+        nc.scalar.activation(warm[:], one[:], ACT.Sqrt)
+
+        w1_codes = sb("w1_codes", PASSES * 2 * H, U8)
+        w1_sc = sb("w1_sc", PASSES * H, U8)
+        nc.vector.tensor_copy(
+            w1_codes[:].bitcast(U16).rearrange("p (g t m) -> p g t m", t=4, m=P),
+            w1_raw[:].bitcast(U16).rearrange("p (g m t) -> p g t m", t=4, m=P),
+        )
+        v_sc = [sb("v_sc%d" % a, S, U8) for a in range(PASSES)]
+        for a in range(PASSES):
+            nc.vector.tensor_copy(v_sc[a][:], tab_sc[:, a * T : (a + 1) * T].indirect(list1[:]))
+
+        nc.vector.tensor_copy(
+            w1_sc[:].rearrange("p (g t m) -> p g t m", t=4, m=P),
+            w1_sc_raw[:].rearrange("p (g m t) -> p g t m", t=4, m=P),
+        )
+        nc.sync.dma_start(list2[:], offs2)
+        nc.gpsimd.dma_start(floor_sb[:], floor.rearrange("(p t) -> p t", t=4))
+        v_codes = [sb("v_codes%d" % a, S, U32) for a in range(PASSES)]
+        nc.vector.tensor_copy(v_codes[0][:], tab[0].bitcast(U32).indirect(list1[:]))
+        for half in range(2):
+            nc.vector.tensor_copy(
+                v_codes[1][:, half * BANK : (half + 1) * BANK],
+                tab[1].bitcast(U32).indirect(list1[:, half * 32 : (half + 1) * 32]),
+            )
+
+        pages = [sb("page%d" % i, T2, F32, tag="page%d" % i) for i in range(2)]
+        for i in range(2):
+            nc.vector.memset(pages[i][:], 0.0)
+
+        rw = [sb("rw%d" % i, 2 * S, F32, tag="rw", bufs=4) for i in range(TILES // 2)]
+
+        def weigh(k):
+            nc.scalar.activation(
+                rw[k // 2][:, (k % 2) * S : (k % 2 + 1) * S], wgs_sb[:], ACT.Copy, scale=rate_sb[:, k : k + 1]
+            )
+
+        kept_rows = kept.rearrange("(b p u e) m -> b u p (e m)", b=PASSES, u=2, e=2)
+        kept_ring = sb("kept_ring", 2 * 2 * T2, F32, tag="big")
+        kept_sb = [kept_ring[:, (pair % 2) * 2 * T2 : (pair % 2 + 1) * 2 * T2] for pair in range(4)]
+
+        def load_kept(pair):
+            nc.sync.dma_start(kept_sb[pair], kept_rows[pair // 2, pair % 2])
+
+        h = {}
+
+        def features(k, banks):
+            b, t = divmod(k, 4)
+            if k < 2:
+                sq = sb("sq%d" % k, S, F32, tag="late_page%d" % k)
+            else:
+                sq = sb("sq%d" % k, S, F32, tag="sq", bufs=2)
+            h[k] = sb("h%d" % k, S, F32, tag="h", bufs=4)
+            for half in range(2):
+                cols = slice(half * BANK, (half + 1) * BANK)
+                acc = bank(banks[half], "a%d_%d" % (k, half))
+                for a in range(PASSES):
+                    c0 = a * H + b * BANK + t * P
+                    nc.tensor.matmul_mx(
+                        out=acc[:],
+                        lhsT=w1_codes[:, 2 * c0 : 2 * (c0 + P)].bitcast(FP4X4),
+                        lhsT_scale=w1_sc[:, c0 : c0 + P],
+                        rhs=v_codes[a][:, cols].bitcast(FP8X4),
+                        rhs_scale=v_sc[a][:, cols],
+                        start=(a == 0),
+                        stop=(a == PASSES - 1),
+                    )
+                nc.scalar.activation(sq[:, cols], acc[:], ACT.Square)
+                if k == 0:
+                    nc.scalar.activation(h[k][:, cols], sq[:, cols], ACT.Sqrt, bias=1.0)
+            if k > 0:
+                nc.scalar.activation(h[k][:], sq[:], ACT.Sqrt, bias=1.0)
+
+        def scatter(k):
+            pieces = 2 if k == 0 else 1
+            n = S // pieces
+            for i in range(pieces):
+                c0 = (k % 2) * S + i * n
+                nc.vector.tensor_tensor(
+                    pages[k % PAGES][:].indirect(list2[:, i * n // 16 : (i + 1) * n // 16]),
+                    h[k][:, i * n : (i + 1) * n],
+                    rw[k // 2][:, c0 : c0 + n],
+                    ALU.mult,
+                )
+
+        fwd_banks, back_banks = [2, 3, 4], [5, 6, 7]
+        turn = {"fwd": 0, "back": 0}
+
+        def take(kind, banks, name):
+            i = turn[kind]
+            turn[kind] = i + 1
+            return bank(banks[i % len(banks)], "%s%d" % (name, i))
+
+        def add_block(dst, k, c):
+            e = k % 2
+            cols = slice(c * P, (c + 1) * P)
+            nc.tensor.matmul(dst, kept_sb[k // 2][:, e * T2 + c * P : e * T2 + (c + 1) * P], ident[:],
+                             start=True, stop=False, is_transpose=True)
+            nc.tensor.matmul(dst, pages[k % PAGES][:, cols], ident[:], start=False, stop=True, is_transpose=True)
+
+        def blend_pair(pair, zt):
+            for c0 in range(0, BLOCKS, 2):
+                f = take("fwd", fwd_banks, "f")
+                for cc in range(2):
+                    for e in range(2):
+                        s0 = (cc * 2 + e) * P
+                        add_block(f[:, s0 : s0 + P], 2 * pair + e, c0 + cc)
+                nc.scalar.copy(
+                    zt[:, c0 * 2 * P : (c0 + 2) * 2 * P].rearrange("m (c p e) -> m c p e", c=2, e=2),
+                    f[:].rearrange("m (c e p) -> m c p e", c=2, e=2),
+                )
+
+        def blend_single(k, zt):
+            for c0 in range(0, BLOCKS, 4):
+                f = take("fwd", fwd_banks, "f")
+                for cc in range(4):
+                    add_block(f[:, cc * P : (cc + 1) * P], k, c0 + cc)
+                nc.scalar.copy(
+                    zt[:, c0 * 2 * P : (c0 + 4) * 2 * P].rearrange("m (x e) -> m x e", e=2)[:, :, 0], f[:]
+                )
+
+        def words(zt, c):
+            return zt[:, c * 2 * P : (c + 1) * 2 * P].bitcast(F32)
+
+        def back_both(zts, dst):
+            for c0 in range(0, BLOCKS, 2):
+                g = take("back", back_banks, "g")
+                for u in range(2):
+                    for cc in range(2):
+                        s0 = (u * 2 + cc) * P
+                        nc.tensor.transpose(g[:, s0 : s0 + P], words(zts[u], c0 + cc), ident[:])
+                nc.scalar.copy(
+                    dst[:, c0 * 4 * P : (c0 + 2) * 4 * P].bitcast(F32).rearrange("p (m u) -> p m u", u=2),
+                    g[:].rearrange("p (u m) -> p m u", u=2),
+                )
+
+        def back_one(zt, dst, u):
+            for c0 in range(0, BLOCKS, 4):
+                g = take("back", back_banks, "g")
+                for cc in range(4):
+                    nc.tensor.transpose(g[:, cc * P : (cc + 1) * P], words(zt, c0 + cc), ident[:])
+                w0 = u * T2 + c0 * P
+                nc.scalar.copy(dst[:, 2 * w0 : 2 * (w0 + BANK)].bitcast(F32), g[:])
+
+        w2_raw = sb("w2_raw", PASSES * 4 * N, F32, tag="w2_raw")
+        nc.sync.dma_start(
+            w2_raw[:].rearrange("p (b x) -> p b x", b=PASSES),
+            w2.rearrange("(b p j) n -> p b (j n)", b=PASSES, j=4),
+        )
+
+        load_kept(0)
+        load_kept(1)
+        weigh(0)
+        weigh(1)
+        features(0, [0, 1])
+        features(1, [0, 1])
+        for k in range(2, TILES):
+            weigh(k)
+        for i in range(2):
+            pages.append(sb("page%d" % (2 + i), T2, F32, tag="late_page%d" % i))
+            nc.gpsimd.memset(pages[2 + i][:], 0.0)
+        features(2, [0, 1])
+        features(3, [0, 1])
+        scatter(0)
+        clock = sb("clock", 2, F32)
+        scatter(1)
+
+        w2_bf = sb("w2_bf", PASSES * 4 * N, BF16, tag="zt1")
+        w2_codes = sb("w2_codes", PASSES * N, U32)
+        w2_sc = sb("w2_sc", PASSES * N, U8)
+        for b in range(PASSES):
+            cols = slice(b * 4 * N, (b + 1) * 4 * N)
+            nc.scalar.copy(
+                w2_bf[:, cols].rearrange("p (t m j) -> p m t j", t=4, j=4),
+                w2_raw[:, cols].rearrange("p (j m t) -> p m t j", t=4, j=4),
+            )
+        nc.vector.quantize_mx(out=w2_codes[:].bitcast(FP8X4), scales=w2_sc[:], in_=w2_bf[:])
+
+        zt = [sb("zt%d" % u, BLOCKS * 2 * P, BF16, tag="zt%d" % u) for u in range(2)]
+        z0 = sb("z0", 4 * T2, BF16)
+        z1_words = sb("z1_words", 4 * T2, BF16)
+
+        features(4, [0, 1])
+        features(5, [0, 1])
+        blend_pair(0, zt[0])
+        load_kept(2)
+        scatter(2)
+        scatter(3)
+        features(6, [fwd_banks[0], fwd_banks[1]])
+        features(7, [fwd_banks[2], fwd_banks[0]])
+        blend_pair(1, zt[1])
+        load_kept(3)
+        back_both(zt, z0)
+        scatter(4)
+        scatter(5)
+        blend_pair(2, zt[0])
+        back_one(zt[0], z1_words, 0)
+        scatter(6)
+        blend_single(6, zt[1])
+        back_one(zt[1], z1_words, 1)
+        scatter(7)
+        nc.gpsimd.tensor_copy(clock[:, 1:2], pages[3][:, 0:1])
+
+        z0_codes = sb("z0_codes", T2, U32)
+        z0_sc = sb("z0_sc", T2, U8)
+        y_codes = sb("y_codes", T2, U32)
+        y_sc = sb("y_sc", T2, U8)
+        y_rows = out_0.rearrange("(p t) m -> p t m", t=4)
+        y_words = out_1[0].rearrange("p m t -> p (m t)").bitcast(I32)
+        last = TILES - 1
+        z1_ring = sb("z1_ring", 2 * 4 * BANK, BF16, tag="zt1")
+        for j in range(CHUNKS):
+            cols = slice(j * BANK, (j + 1) * BANK)
+            w0 = T2 + j * BANK
+            nc.vector.tensor_tensor(
+                z1_words[:, 2 * w0 : 2 * (w0 + BANK)].rearrange("p (m e) -> p m e", e=2)[:, :, 1],
+                pages[last % PAGES][:, cols],
+                kept_sb[last // 2][:, w0 : w0 + BANK],
+                ALU.add,
+            )
+            z1 = z1_ring[:, (j % 2) * 4 * BANK : (j % 2 + 1) * 4 * BANK]
+            nc.scalar.copy(
+                z1.bitcast(F32).rearrange("p (m u) -> p m u", u=2),
+                z1_words[:].bitcast(F32).rearrange("p (u m) -> p m u", u=2)[:, cols, :],
+            )
+            nc.vector.quantize_mx(
+                out=z0_codes[:, cols].bitcast(FP8X4), scales=z0_sc[:, cols], in_=z0[:, 4 * j * BANK : 4 * (j + 1) * BANK]
+            )
+            z1_codes = sb("z1_codes%d" % j, BANK, U32, tag="z1c", bufs=2)
+            z1_sc = sb("z1_sc%d" % j, BANK, U8, tag="z1s", bufs=2)
+            nc.vector.quantize_mx(out=z1_codes[:].bitcast(FP8X4), scales=z1_sc[:], in_=z1)
+            y = sb("y%d" % j, 4 * BANK, F32, tag="rw", bufs=4)
+            for t in range(4):
+                acc = bank(4 * (j % 2) + t, "y%d_%d" % (j, t))
+                moving = [(z1_codes[:], z1_sc[:], 1), (z0_codes[:, cols], z0_sc[:, cols], 0)]
+                for i, (codes, scales, b) in enumerate(moving):
+                    c0 = b * N + t * P
+                    nc.tensor.matmul_mx(
+                        out=acc[:],
+                        lhsT=w2_codes[:, c0 : c0 + P].bitcast(FP8X4),
+                        lhsT_scale=w2_sc[:, c0 : c0 + P],
+                        rhs=codes.bitcast(FP8X4),
+                        rhs_scale=scales,
+                        start=(i == 0),
+                        stop=(i == PASSES - 1),
+                    )
+                nc.vector.tensor_scalar_max(y[:, t * BANK : (t + 1) * BANK], acc[:], floor_sb[:, t : t + 1])
+            nc.sync.dma_start(y_rows[:, :, cols], y[:].rearrange("p (t m) -> p t m", t=4))
+            y_bf = sb("y_bf%d" % j, 4 * BANK, BF16, tag="h", bufs=4)
+            nc.scalar.copy(
+                y_bf[:].rearrange("p (m t) -> p m t", t=4), y[:].rearrange("p (t m) -> p m t", t=4)
+            )
+            nc.vector.quantize_mx(out=y_codes[:, cols].bitcast(FP8X4), scales=y_sc[:, cols], in_=y_bf[:])
+            nc.sync.dma_start(y_words[:, cols], y_codes[:, cols].bitcast(I32))
+        for q in range(4):
+            queue = nc.sync if q % 2 == 0 else nc.scalar
+            queue.dma_start(out_2[0, 4 * q : 4 * q + 4, :].bitcast(I32), y_sc[32 * q : 32 * q + 4, :].bitcast(I32))

@@ -25,6 +25,7 @@ PAGES = 4
 BLOCKS = T2 // P
 CHUNKS = T2 // BANK
 AL = 64
+SHARE = 160
 
 
 def tile_list_berth_page_nowcast_kernel(
@@ -188,8 +189,8 @@ def tile_list_berth_page_nowcast_kernel(
                              start=True, stop=False, is_transpose=True)
             nc.tensor.matmul(dst, pages[k % PAGES][:, cols], ident[:], start=False, stop=True, is_transpose=True)
 
-        def blend_pair(pair, zt):
-            for c0 in range(0, BLOCKS, 2):
+        def blend_pair(pair, zt, first, last):
+            for c0 in range(first, last, 2):
                 f = take("fwd", fwd_banks, "f")
                 for cc in range(2):
                     for e in range(2):
@@ -198,15 +199,6 @@ def tile_list_berth_page_nowcast_kernel(
                 nc.scalar.copy(
                     zt[:, c0 * 2 * P : (c0 + 2) * 2 * P].rearrange("m (c p e) -> m c p e", c=2, e=2),
                     f[:].rearrange("m (c e p) -> m c p e", c=2, e=2),
-                )
-
-        def blend_single(k, zt):
-            for c0 in range(0, BLOCKS, 4):
-                f = take("fwd", fwd_banks, "f")
-                for cc in range(4):
-                    add_block(f[:, cc * P : (cc + 1) * P], k, c0 + cc)
-                nc.scalar.copy(
-                    zt[:, c0 * 2 * P : (c0 + 4) * 2 * P].rearrange("m (x e) -> m x e", e=2)[:, :, 0], f[:]
                 )
 
         def words(zt, c):
@@ -252,7 +244,6 @@ def tile_list_berth_page_nowcast_kernel(
         features(2, [0, 1])
         features(3, [0, 1])
         scatter(0)
-        clock = sb("clock", 2, F32)
         scatter(1)
 
         w2_bf = sb("w2_bf", PASSES * 4 * N, BF16, tag="zt1")
@@ -272,24 +263,22 @@ def tile_list_berth_page_nowcast_kernel(
 
         features(4, [0, 1])
         features(5, [0, 1])
-        blend_pair(0, zt[0])
+        blend_pair(0, zt[0], 0, BLOCKS)
         load_kept(2)
         scatter(2)
         scatter(3)
-        features(6, [fwd_banks[0], fwd_banks[1]])
+        features(6, [fwd_banks[2], fwd_banks[0]])
+        blend_pair(1, zt[1], 0, 4)
         features(7, [fwd_banks[2], fwd_banks[0]])
-        blend_pair(1, zt[1])
+        blend_pair(1, zt[1], 4, BLOCKS)
         load_kept(3)
         back_both(zt, z0)
         scatter(4)
         scatter(5)
-        blend_pair(2, zt[0])
+        blend_pair(2, zt[0], 0, BLOCKS)
         back_one(zt[0], z1_words, 0)
         scatter(6)
-        blend_single(6, zt[1])
-        back_one(zt[1], z1_words, 1)
         scatter(7)
-        nc.gpsimd.tensor_copy(clock[:, 1:2], pages[3][:, 0:1])
 
         z0_codes = sb("z0_codes", T2, U32)
         z0_sc = sb("z0_sc", T2, U8)
@@ -298,16 +287,17 @@ def tile_list_berth_page_nowcast_kernel(
         y_rows = out_0.rearrange("(p t) m -> p t m", t=4)
         y_words = out_1[0].rearrange("p m t -> p (m t)").bitcast(I32)
         last = TILES - 1
-        z1_ring = sb("z1_ring", 2 * 4 * BANK, BF16, tag="zt1")
+        z1_ring = sb("z1_ring", 2 * 4 * BANK, BF16, tag="zt0")
         for j in range(CHUNKS):
             cols = slice(j * BANK, (j + 1) * BANK)
             w0 = T2 + j * BANK
-            nc.vector.tensor_tensor(
-                z1_words[:, 2 * w0 : 2 * (w0 + BANK)].rearrange("p (m e) -> p m e", e=2)[:, :, 1],
-                pages[last % PAGES][:, cols],
-                kept_sb[last // 2][:, w0 : w0 + BANK],
-                ALU.add,
-            )
+            for e in range(2):
+                nc.vector.tensor_tensor(
+                    z1_words[:, 2 * w0 : 2 * (w0 + BANK)].rearrange("p (m e) -> p m e", e=2)[:, :, e],
+                    pages[(last - 1 + e) % PAGES][:, cols],
+                    kept_sb[last // 2][:, e * T2 + j * BANK : e * T2 + (j + 1) * BANK],
+                    ALU.add,
+                )
             z1 = z1_ring[:, (j % 2) * 4 * BANK : (j % 2 + 1) * 4 * BANK]
             nc.scalar.copy(
                 z1.bitcast(F32).rearrange("p (m u) -> p m u", u=2),
@@ -334,12 +324,22 @@ def tile_list_berth_page_nowcast_kernel(
                         start=(i == 0),
                         stop=(i == PASSES - 1),
                     )
-                nc.vector.tensor_scalar_max(y[:, t * BANK : (t + 1) * BANK], acc[:], floor_sb[:, t : t + 1])
+                y_t = y[:, t * BANK : (t + 1) * BANK]
+                if t % 2 == 0 and j < CHUNKS - 1:
+                    raw = sb("raw%d_%d" % (j, t), BANK, F32, tag="raw", bufs=2)
+                    nc.scalar.copy(raw[:], acc[:])
+                    nc.vector.tensor_scalar_max(y_t, raw[:], floor_sb[:, t : t + 1])
+                else:
+                    nc.vector.tensor_scalar_max(y_t, acc[:], floor_sb[:, t : t + 1])
             nc.sync.dma_start(y_rows[:, :, cols], y[:].rearrange("p (t m) -> p t m", t=4))
             y_bf = sb("y_bf%d" % j, 4 * BANK, BF16, tag="h", bufs=4)
-            nc.scalar.copy(
-                y_bf[:].rearrange("p (m t) -> p m t", t=4), y[:].rearrange("p (t m) -> p m t", t=4)
-            )
+            rounded = y_bf[:].rearrange("p (m t) -> p m t", t=4)
+            by_column = y[:].rearrange("p (t m) -> p m t", t=4)
+            if j < CHUNKS - 1:
+                nc.scalar.copy(rounded, by_column)
+            else:
+                nc.scalar.copy(rounded[:, :SHARE, :], by_column[:, :SHARE, :])
+                nc.vector.tensor_copy(rounded[:, SHARE:, :], by_column[:, SHARE:, :])
             nc.vector.quantize_mx(out=y_codes[:, cols].bitcast(FP8X4), scales=y_sc[:, cols], in_=y_bf[:])
             nc.sync.dma_start(y_words[:, cols], y_codes[:, cols].bitcast(I32))
         for q in range(4):

@@ -25,7 +25,7 @@ PAGES = 4
 BLOCKS = T2 // P
 CHUNKS = T2 // BANK
 AL = 64
-SHARE = 160
+SHARE = 44
 
 
 def tile_list_berth_page_nowcast_kernel(
@@ -53,16 +53,18 @@ def tile_list_berth_page_nowcast_kernel(
         warm = sb("warm", 1, F32)
         ident = sb("ident", P, F32)
 
-        tab_sc = sb("tab_sc", PASSES * T, U8, tag="w2_raw")
+        tab_sc = sb("tab_sc", T, U8, tag="w2_raw")
         seed = sb("seed", 1, F32, tag="big")
         wgs_sb = sb("wgs_sb", S, F32, tag="sq", bufs=2)
         w1_raw = sb("w1_raw", PASSES * 2 * H, U8, tag="page0")
         w1_sc_raw = sb("w1_sc_raw", PASSES * H, U8, tag="page1")
+        v_sc1 = sb("v_sc1", S, U8)
 
         nc.vector.memset(tab_sc[:].bitcast(I32), 0)
         nc.vector.memset(seed[:], 1.0)
         nc.vector.tensor_copy(one[:], seed[:])
         nc.vector.memset(w1_sc_raw[:].bitcast(I32), 0)
+        nc.vector.memset(v_sc1[:].bitcast(I32), 0)
 
         nc.sync.dma_start(list1[:], offs)
         nc.sync.dma_start(
@@ -71,8 +73,7 @@ def tile_list_berth_page_nowcast_kernel(
         )
         for q in range(4):
             nc.sync.dma_start(
-                tab_sc[32 * q : 32 * q + 4, :].bitcast(I32).rearrange("r (a c) -> r a c", a=PASSES),
-                tab_scales[:, 4 * q : 4 * q + 4, :].bitcast(I32).rearrange("a r c -> r a c"),
+                tab_sc[32 * q : 32 * q + 8, :].bitcast(I32), tab_scales[:, 4 * q : 4 * q + 4, :].bitcast(I32)
             )
         for q in range(4):
             nc.scalar.dma_start(
@@ -97,9 +98,11 @@ def tile_list_berth_page_nowcast_kernel(
             w1_codes[:].bitcast(U16).rearrange("p (g t m) -> p g t m", t=4, m=P),
             w1_raw[:].bitcast(U16).rearrange("p (g m t) -> p g t m", t=4, m=P),
         )
-        v_sc = [sb("v_sc%d" % a, S, U8) for a in range(PASSES)]
-        for a in range(PASSES):
-            nc.vector.tensor_copy(v_sc[a][:], tab_sc[:, a * T : (a + 1) * T].indirect(list1[:]))
+        v_sc0 = sb("v_sc0", S, U8)
+        nc.vector.tensor_copy(v_sc0[:], tab_sc[:].indirect(list1[:]))
+        for r in range(4):
+            nc.sync.dma_start(v_sc1[r:P:32, :].bitcast(I32), v_sc0[4 + r : P : 32, :].bitcast(I32))
+        v_sc = [v_sc0, v_sc1]
 
         nc.vector.tensor_copy(
             w1_sc[:].rearrange("p (g t m) -> p g t m", t=4, m=P),
@@ -115,8 +118,8 @@ def tile_list_berth_page_nowcast_kernel(
                 tab[1].bitcast(U32).indirect(list1[:, half * 32 : (half + 1) * 32]),
             )
 
-        pages = [sb("page%d" % i, T2, F32, tag="page%d" % i) for i in range(2)]
-        for i in range(2):
+        pages = [sb("page%d" % i, T2, F32, tag="page%d" % i) for i in range(PAGES)]
+        for i in range(PAGES):
             nc.vector.memset(pages[i][:], 0.0)
 
         rw = [sb("rw%d" % i, 2 * S, F32, tag="rw", bufs=4) for i in range(TILES // 2)]
@@ -137,10 +140,7 @@ def tile_list_berth_page_nowcast_kernel(
 
         def features(k, banks):
             b, t = divmod(k, 4)
-            if k < 2:
-                sq = sb("sq%d" % k, S, F32, tag="late_page%d" % k)
-            else:
-                sq = sb("sq%d" % k, S, F32, tag="sq", bufs=2)
+            sq = sb("sq%d" % k, S, F32, tag="sq", bufs=2)
             h[k] = sb("h%d" % k, S, F32, tag="h", bufs=4)
             for half in range(2):
                 cols = slice(half * BANK, (half + 1) * BANK)
@@ -189,8 +189,8 @@ def tile_list_berth_page_nowcast_kernel(
                              start=True, stop=False, is_transpose=True)
             nc.tensor.matmul(dst, pages[k % PAGES][:, cols], ident[:], start=False, stop=True, is_transpose=True)
 
-        def blend_pair(pair, zt, first, last):
-            for c0 in range(first, last, 2):
+        def blend_pair(pair, zt):
+            for c0 in range(0, BLOCKS, 2):
                 f = take("fwd", fwd_banks, "f")
                 for cc in range(2):
                     for e in range(2):
@@ -199,6 +199,15 @@ def tile_list_berth_page_nowcast_kernel(
                 nc.scalar.copy(
                     zt[:, c0 * 2 * P : (c0 + 2) * 2 * P].rearrange("m (c p e) -> m c p e", c=2, e=2),
                     f[:].rearrange("m (c e p) -> m c p e", c=2, e=2),
+                )
+
+        def blend_single(k, zt):
+            for c0 in range(0, BLOCKS, 4):
+                f = take("fwd", fwd_banks, "f")
+                for cc in range(4):
+                    add_block(f[:, cc * P : (cc + 1) * P], k, c0 + cc)
+                nc.scalar.copy(
+                    zt[:, c0 * 2 * P : (c0 + 4) * 2 * P].rearrange("m (x e) -> m x e", e=2)[:, :, 0], f[:]
                 )
 
         def words(zt, c):
@@ -238,9 +247,6 @@ def tile_list_berth_page_nowcast_kernel(
         features(1, [0, 1])
         for k in range(2, TILES):
             weigh(k)
-        for i in range(2):
-            pages.append(sb("page%d" % (2 + i), T2, F32, tag="late_page%d" % i))
-            nc.gpsimd.memset(pages[2 + i][:], 0.0)
         features(2, [0, 1])
         features(3, [0, 1])
         scatter(0)
@@ -252,8 +258,8 @@ def tile_list_berth_page_nowcast_kernel(
         for b in range(PASSES):
             cols = slice(b * 4 * N, (b + 1) * 4 * N)
             nc.scalar.copy(
-                w2_bf[:, cols].rearrange("p (t m j) -> p m t j", t=4, j=4),
-                w2_raw[:, cols].rearrange("p (j m t) -> p m t j", t=4, j=4),
+                w2_bf[:, cols].rearrange("p (t m j) -> p m j t", t=4, j=4),
+                w2_raw[:, cols].rearrange("p (j m t) -> p m j t", t=4, j=4),
             )
         nc.vector.quantize_mx(out=w2_codes[:].bitcast(FP8X4), scales=w2_sc[:], in_=w2_bf[:])
 
@@ -263,21 +269,22 @@ def tile_list_berth_page_nowcast_kernel(
 
         features(4, [0, 1])
         features(5, [0, 1])
-        blend_pair(0, zt[0], 0, BLOCKS)
+        blend_pair(0, zt[0])
         load_kept(2)
         scatter(2)
         scatter(3)
-        features(6, [fwd_banks[2], fwd_banks[0]])
-        blend_pair(1, zt[1], 0, 4)
+        features(6, [fwd_banks[0], fwd_banks[1]])
         features(7, [fwd_banks[2], fwd_banks[0]])
-        blend_pair(1, zt[1], 4, BLOCKS)
+        blend_pair(1, zt[1])
         load_kept(3)
         back_both(zt, z0)
         scatter(4)
         scatter(5)
-        blend_pair(2, zt[0], 0, BLOCKS)
+        blend_pair(2, zt[0])
         back_one(zt[0], z1_words, 0)
         scatter(6)
+        blend_single(6, zt[1])
+        back_one(zt[1], z1_words, 1)
         scatter(7)
 
         z0_codes = sb("z0_codes", T2, U32)
@@ -287,17 +294,16 @@ def tile_list_berth_page_nowcast_kernel(
         y_rows = out_0.rearrange("(p t) m -> p t m", t=4)
         y_words = out_1[0].rearrange("p m t -> p (m t)").bitcast(I32)
         last = TILES - 1
-        z1_ring = sb("z1_ring", 2 * 4 * BANK, BF16, tag="zt0")
+        z1_ring = sb("z1_ring", 2 * 4 * BANK, BF16, tag="zt1")
         for j in range(CHUNKS):
             cols = slice(j * BANK, (j + 1) * BANK)
             w0 = T2 + j * BANK
-            for e in range(2):
-                nc.vector.tensor_tensor(
-                    z1_words[:, 2 * w0 : 2 * (w0 + BANK)].rearrange("p (m e) -> p m e", e=2)[:, :, e],
-                    pages[(last - 1 + e) % PAGES][:, cols],
-                    kept_sb[last // 2][:, e * T2 + j * BANK : e * T2 + (j + 1) * BANK],
-                    ALU.add,
-                )
+            nc.vector.tensor_tensor(
+                z1_words[:, 2 * w0 : 2 * (w0 + BANK)].rearrange("p (m e) -> p m e", e=2)[:, :, 1],
+                pages[last % PAGES][:, cols],
+                kept_sb[last // 2][:, w0 : w0 + BANK],
+                ALU.add,
+            )
             z1 = z1_ring[:, (j % 2) * 4 * BANK : (j % 2 + 1) * 4 * BANK]
             nc.scalar.copy(
                 z1.bitcast(F32).rearrange("p (m u) -> p m u", u=2),
@@ -331,15 +337,18 @@ def tile_list_berth_page_nowcast_kernel(
                     nc.vector.tensor_scalar_max(y_t, raw[:], floor_sb[:, t : t + 1])
                 else:
                     nc.vector.tensor_scalar_max(y_t, acc[:], floor_sb[:, t : t + 1])
-            nc.sync.dma_start(y_rows[:, :, cols], y[:].rearrange("p (t m) -> p t m", t=4))
+                if j == CHUNKS - 1:
+                    nc.sync.dma_start(y_rows[:, t, cols], y_t)
+            if j < CHUNKS - 1:
+                nc.sync.dma_start(y_rows[:, :, cols], y[:].rearrange("p (t m) -> p t m", t=4))
             y_bf = sb("y_bf%d" % j, 4 * BANK, BF16, tag="h", bufs=4)
-            rounded = y_bf[:].rearrange("p (m t) -> p m t", t=4)
-            by_column = y[:].rearrange("p (t m) -> p m t", t=4)
+            rounded = y_bf[:].rearrange("p (c i t) -> p c t i", t=4, i=4)
+            by_column = y[:].rearrange("p (t c i) -> p c t i", t=4, i=4)
             if j < CHUNKS - 1:
                 nc.scalar.copy(rounded, by_column)
             else:
-                nc.scalar.copy(rounded[:, :SHARE, :], by_column[:, :SHARE, :])
-                nc.vector.tensor_copy(rounded[:, SHARE:, :], by_column[:, SHARE:, :])
+                nc.scalar.copy(rounded[:, :SHARE], by_column[:, :SHARE])
+                nc.vector.tensor_copy(rounded[:, SHARE:], by_column[:, SHARE:])
             nc.vector.quantize_mx(out=y_codes[:, cols].bitcast(FP8X4), scales=y_sc[:, cols], in_=y_bf[:])
             nc.sync.dma_start(y_words[:, cols], y_codes[:, cols].bitcast(I32))
         for q in range(4):

@@ -18,14 +18,21 @@ ACT = mybir.ActivationFunctionType
 ALU = mybir.AluOpType
 
 P = 128
+PACK = 4
 BANK = 512
 PASSES = 2
-TILES = 8
+TILES = H // P
 PAGES = 4
 BLOCKS = T2 // P
 CHUNKS = T2 // BANK
-AL = 64
-SHARE = 44
+GROUP = 16
+QUADS = 4
+ALIGN = 64
+FIRST_PIECES = [(0, 128), (128, 512), (512, 1024)]
+SCALAR_RUNS = 44
+FEATURE_BANKS = [0, 1]
+SUM_BANKS = [2, 3, 4]
+BACK_BANKS = [5, 6, 7]
 
 
 def tile_list_berth_page_nowcast_kernel(
@@ -34,93 +41,88 @@ def tile_list_berth_page_nowcast_kernel(
     nc = tc.nc
     with ExitStack() as ctx:
         held = ctx.enter_context(tc.tile_pool(name="held", bufs=1))
-        ring = ctx.enter_context(tc.tile_pool(name="ring", bufs=1))
+        shared = ctx.enter_context(tc.tile_pool(name="shared", bufs=1))
         psum = ctx.enter_context(tc.psum_pool(name="psum", bufs=1))
 
         def sb(name, cols, dtype, tag=None, bufs=1):
             if tag is None:
-                return held.tile([P, cols], dtype, name=name, align_bytes=AL)
-            return ring.tile([P, cols], dtype, name=name, tag=tag, bufs=bufs, align_bytes=AL)
+                return held.tile([P, cols], dtype, name=name, align_bytes=ALIGN)
+            return shared.tile([P, cols], dtype, name=name, tag=tag, bufs=bufs, align_bytes=ALIGN)
 
         def bank(i, name):
             return psum.tile([P, BANK], F32, name=name, tag="bank%d" % i)
 
-        list1 = held.tile([P, S // 16], U16, name="list1")
-        list2 = held.tile([P, S // 16], U16, name="list2")
+        list1 = held.tile([P, S // GROUP], U16, name="list1")
+        list2 = held.tile([P, S // GROUP], U16, name="list2")
         rate_sb = sb("rate_sb", TILES, F32)
-        floor_sb = sb("floor_sb", 4, F32)
+        floor_sb = sb("floor_sb", PACK, F32)
         one = sb("one", 1, F32)
-        warm = sb("warm", 1, F32)
+        unit = sb("unit", 1, F32)
         ident = sb("ident", P, F32)
-
         tab_sc = sb("tab_sc", T, U8, tag="w2_raw")
-        seed = sb("seed", 1, F32, tag="big")
         wgs_sb = sb("wgs_sb", S, F32, tag="sq", bufs=2)
         w1_raw = sb("w1_raw", PASSES * 2 * H, U8, tag="page0")
         w1_sc_raw = sb("w1_sc_raw", PASSES * H, U8, tag="page1")
         v_sc1 = sb("v_sc1", S, U8)
 
         nc.vector.memset(tab_sc[:].bitcast(I32), 0)
-        nc.vector.memset(seed[:], 1.0)
-        nc.vector.tensor_copy(one[:], seed[:])
         nc.vector.memset(w1_sc_raw[:].bitcast(I32), 0)
+        nc.vector.memset(one[:], 1.0)
         nc.vector.memset(v_sc1[:].bitcast(I32), 0)
 
         nc.sync.dma_start(list1[:], offs)
+        nc.sync.dma_start(list2[:], offs2)
         nc.sync.dma_start(
             w1_raw[:].bitcast(I32).rearrange("p (a c) -> p a c", a=PASSES),
             w1_words.bitcast(I32).rearrange("a p c -> p a c"),
         )
-        for q in range(4):
+        for q in range(QUADS):
             nc.sync.dma_start(
                 tab_sc[32 * q : 32 * q + 8, :].bitcast(I32), tab_scales[:, 4 * q : 4 * q + 4, :].bitcast(I32)
             )
-        for q in range(4):
+        for q in range(QUADS):
             nc.scalar.dma_start(
                 w1_sc_raw[32 * q : 32 * q + 4, :].bitcast(I32).rearrange("r (a c) -> r a c", a=PASSES),
                 w1_scales[:, 4 * q : 4 * q + 4, :].bitcast(I32).rearrange("a r c -> r a c"),
             )
         nc.sync.dma_start(wgs_sb[:], wgs)
-        tab_sb = sb("tab_sb", PASSES * T, I32, tag="big")
-        tab = [tab_sb[:, a * T : (a + 1) * T] for a in range(PASSES)]
+        tab = [sb("tab%d" % a, T, I32, tag="big%d" % a) for a in range(PASSES)]
         for a in range(PASSES):
-            nc.sync.dma_start(tab[a], tab_words[a].rearrange("p c i -> p (c i)").bitcast(I32))
-        nc.gpsimd.dma_start(
-            rate_sb[:].rearrange("p (b t) -> p b t", b=PASSES), rate.rearrange("(b p t) -> p b t", b=PASSES, t=4)
+            nc.sync.dma_start(tab[a][:], tab_words[a].rearrange("p c i -> p (c i)").bitcast(I32))
+        nc.scalar.dma_start(
+            rate_sb[:].rearrange("p (b t) -> p b t", b=PASSES), rate.rearrange("(b p t) -> p b t", b=PASSES, t=PACK)
         )
 
         make_identity(nc, ident[:])
-        nc.scalar.activation(warm[:], one[:], ACT.Sqrt)
+        nc.scalar.activation(unit[:], one[:], ACT.Sqrt)
 
         w1_codes = sb("w1_codes", PASSES * 2 * H, U8)
         w1_sc = sb("w1_sc", PASSES * H, U8)
         nc.vector.tensor_copy(
-            w1_codes[:].bitcast(U16).rearrange("p (g t m) -> p g t m", t=4, m=P),
-            w1_raw[:].bitcast(U16).rearrange("p (g m t) -> p g t m", t=4, m=P),
+            w1_codes[:].bitcast(U16).rearrange("p (g t m) -> p g t m", t=PACK, m=P),
+            w1_raw[:].bitcast(U16).rearrange("p (g m t) -> p g t m", t=PACK, m=P),
         )
+
         v_sc0 = sb("v_sc0", S, U8)
         nc.vector.tensor_copy(v_sc0[:], tab_sc[:].indirect(list1[:]))
-        for r in range(4):
-            nc.sync.dma_start(v_sc1[r:P:32, :].bitcast(I32), v_sc0[4 + r : P : 32, :].bitcast(I32))
+        for i in range(4):
+            nc.sync.dma_start(v_sc1[i:P:32, :].bitcast(I32), v_sc0[4 + i : P : 32, :].bitcast(I32))
         v_sc = [v_sc0, v_sc1]
-
         nc.vector.tensor_copy(
-            w1_sc[:].rearrange("p (g t m) -> p g t m", t=4, m=P),
-            w1_sc_raw[:].rearrange("p (g m t) -> p g t m", t=4, m=P),
+            w1_sc[:].rearrange("p (g t m) -> p g t m", t=PACK, m=P),
+            w1_sc_raw[:].rearrange("p (g m t) -> p g t m", t=PACK, m=P),
         )
-        nc.sync.dma_start(list2[:], offs2)
-        nc.gpsimd.dma_start(floor_sb[:], floor.rearrange("(p t) -> p t", t=4))
+        nc.gpsimd.dma_start(floor_sb[:], floor.rearrange("(p t) -> p t", t=PACK))
         v_codes = [sb("v_codes%d" % a, S, U32) for a in range(PASSES)]
-        nc.vector.tensor_copy(v_codes[0][:], tab[0].bitcast(U32).indirect(list1[:]))
-        for half in range(2):
+        nc.vector.tensor_copy(v_codes[0][:], tab[0][:].bitcast(U32).indirect(list1[:]))
+        for lo in range(0, S, BANK):
             nc.vector.tensor_copy(
-                v_codes[1][:, half * BANK : (half + 1) * BANK],
-                tab[1].bitcast(U32).indirect(list1[:, half * 32 : (half + 1) * 32]),
+                v_codes[1][:, lo : lo + BANK],
+                tab[1][:].bitcast(U32).indirect(list1[:, lo // GROUP : (lo + BANK) // GROUP]),
             )
 
-        pages = [sb("page%d" % i, T2, F32, tag="page%d" % i) for i in range(PAGES)]
-        for i in range(PAGES):
-            nc.vector.memset(pages[i][:], 0.0)
+        pages = [sb("page0", T2, F32, tag="page0")]
+        nc.vector.memset(pages[0][:], 0.0)
 
         rw = [sb("rw%d" % i, 2 * S, F32, tag="rw", bufs=4) for i in range(TILES // 2)]
 
@@ -130,84 +132,91 @@ def tile_list_berth_page_nowcast_kernel(
             )
 
         kept_rows = kept.rearrange("(b p u e) m -> b u p (e m)", b=PASSES, u=2, e=2)
-        kept_ring = sb("kept_ring", 2 * 2 * T2, F32, tag="big")
-        kept_sb = [kept_ring[:, (pair % 2) * 2 * T2 : (pair % 2 + 1) * 2 * T2] for pair in range(4)]
+        kept_sb = {}
 
         def load_kept(pair):
-            nc.sync.dma_start(kept_sb[pair], kept_rows[pair // 2, pair % 2])
+            kept_sb[pair] = sb("kept%d" % pair, 2 * T2, F32, tag="big%d" % (pair % 2))
+            nc.sync.dma_start(kept_sb[pair][:], kept_rows[pair // 2, pair % 2])
 
         h = {}
 
         def features(k, banks):
-            b, t = divmod(k, 4)
-            sq = sb("sq%d" % k, S, F32, tag="sq", bufs=2)
+            b, t = divmod(k, PACK)
+            if k < PAGES - 1:
+                sq = sb("sq%d" % k, S, F32, tag="page%d" % (k + 1))
+            elif k == PAGES - 1:
+                sq = sb("sq%d" % k, S, F32, tag="zt1")
+            else:
+                sq = sb("sq%d" % k, S, F32, tag="sq", bufs=2)
             h[k] = sb("h%d" % k, S, F32, tag="h", bufs=4)
-            for half in range(2):
-                cols = slice(half * BANK, (half + 1) * BANK)
-                acc = bank(banks[half], "a%d_%d" % (k, half))
-                for a in range(PASSES):
-                    c0 = a * H + b * BANK + t * P
-                    nc.tensor.matmul_mx(
-                        out=acc[:],
-                        lhsT=w1_codes[:, 2 * c0 : 2 * (c0 + P)].bitcast(FP4X4),
-                        lhsT_scale=w1_sc[:, c0 : c0 + P],
-                        rhs=v_codes[a][:, cols].bitcast(FP8X4),
-                        rhs_scale=v_sc[a][:, cols],
-                        start=(a == 0),
-                        stop=(a == PASSES - 1),
-                    )
-                nc.scalar.activation(sq[:, cols], acc[:], ACT.Square)
+            spans = FIRST_PIECES if k == 0 else [(0, BANK), (BANK, S)]
+            for i, (lo, hi) in enumerate(spans):
+                acc = bank(banks[i], "a%d_%d" % (k, i))
+                width = BANK if hi - lo == BANK else P
+                for n0 in range(lo, hi, width):
+                    for a in range(PASSES):
+                        c0 = a * H + b * BANK + t * P
+                        nc.tensor.matmul_mx(
+                            out=acc[:, n0 - lo : n0 - lo + width],
+                            lhsT=w1_codes[:, 2 * c0 : 2 * (c0 + P)].bitcast(FP4X4),
+                            lhsT_scale=w1_sc[:, c0 : c0 + P],
+                            rhs=v_codes[a][:, n0 : n0 + width].bitcast(FP8X4),
+                            rhs_scale=v_sc[a][:, n0 : n0 + width],
+                            start=(a == 0),
+                            stop=(a == PASSES - 1),
+                        )
+                nc.scalar.activation(sq[:, lo:hi], acc[:, : hi - lo], ACT.Square)
                 if k == 0:
-                    nc.scalar.activation(h[k][:, cols], sq[:, cols], ACT.Sqrt, bias=1.0)
+                    nc.scalar.activation(h[k][:, lo:hi], sq[:, lo:hi], ACT.Sqrt, bias=unit[:])
             if k > 0:
-                nc.scalar.activation(h[k][:], sq[:], ACT.Sqrt, bias=1.0)
+                nc.scalar.activation(h[k][:], sq[:], ACT.Sqrt, bias=unit[:])
+            if k < PAGES - 1:
+                pages.append(sb("page%d" % (k + 1), T2, F32, tag="page%d" % (k + 1)))
+                nc.gpsimd.memset(pages[k + 1][:], 0.0)
 
         def scatter(k):
-            pieces = 2 if k == 0 else 1
-            n = S // pieces
-            for i in range(pieces):
-                c0 = (k % 2) * S + i * n
+            c0 = (k % 2) * S
+            for lo, hi in FIRST_PIECES if k == 0 else [(0, S)]:
                 nc.vector.tensor_tensor(
-                    pages[k % PAGES][:].indirect(list2[:, i * n // 16 : (i + 1) * n // 16]),
-                    h[k][:, i * n : (i + 1) * n],
-                    rw[k // 2][:, c0 : c0 + n],
+                    pages[k % PAGES][:].indirect(list2[:, lo // GROUP : hi // GROUP]),
+                    h[k][:, lo:hi],
+                    rw[k // 2][:, c0 + lo : c0 + hi],
                     ALU.mult,
                 )
 
-        fwd_banks, back_banks = [2, 3, 4], [5, 6, 7]
-        turn = {"fwd": 0, "back": 0}
+        turn = {"sum": 0, "back": 0}
 
-        def take(kind, banks, name):
+        def take(kind, banks):
             i = turn[kind]
             turn[kind] = i + 1
-            return bank(banks[i % len(banks)], "%s%d" % (name, i))
+            return bank(banks[i % len(banks)], "%s%d" % (kind, i))
 
         def add_block(dst, k, c):
-            e = k % 2
-            cols = slice(c * P, (c + 1) * P)
-            nc.tensor.matmul(dst, kept_sb[k // 2][:, e * T2 + c * P : e * T2 + (c + 1) * P], ident[:],
-                             start=True, stop=False, is_transpose=True)
-            nc.tensor.matmul(dst, pages[k % PAGES][:, cols], ident[:], start=False, stop=True, is_transpose=True)
+            k0 = (k % 2) * T2 + c * P
+            nc.tensor.matmul(dst, kept_sb[k // 2][:, k0 : k0 + P], ident[:], start=True, stop=False, is_transpose=True)
+            nc.tensor.matmul(
+                dst, pages[k % PAGES][:, c * P : (c + 1) * P], ident[:], start=False, stop=True, is_transpose=True
+            )
 
         def blend_pair(pair, zt):
             for c0 in range(0, BLOCKS, 2):
-                f = take("fwd", fwd_banks, "f")
+                sums = take("sum", SUM_BANKS)
                 for cc in range(2):
                     for e in range(2):
                         s0 = (cc * 2 + e) * P
-                        add_block(f[:, s0 : s0 + P], 2 * pair + e, c0 + cc)
+                        add_block(sums[:, s0 : s0 + P], 2 * pair + e, c0 + cc)
                 nc.scalar.copy(
                     zt[:, c0 * 2 * P : (c0 + 2) * 2 * P].rearrange("m (c p e) -> m c p e", c=2, e=2),
-                    f[:].rearrange("m (c e p) -> m c p e", c=2, e=2),
+                    sums[:].rearrange("m (c e p) -> m c p e", c=2, e=2),
                 )
 
-        def blend_single(k, zt):
+        def blend_low(k, zt):
             for c0 in range(0, BLOCKS, 4):
-                f = take("fwd", fwd_banks, "f")
+                sums = take("sum", SUM_BANKS)
                 for cc in range(4):
-                    add_block(f[:, cc * P : (cc + 1) * P], k, c0 + cc)
+                    add_block(sums[:, cc * P : (cc + 1) * P], k, c0 + cc)
                 nc.scalar.copy(
-                    zt[:, c0 * 2 * P : (c0 + 4) * 2 * P].rearrange("m (x e) -> m x e", e=2)[:, :, 0], f[:]
+                    zt[:, c0 * 2 * P : (c0 + 4) * 2 * P].rearrange("m (x e) -> m x e", e=2)[:, :, 0], sums[:]
                 )
 
         def words(zt, c):
@@ -215,66 +224,66 @@ def tile_list_berth_page_nowcast_kernel(
 
         def back_both(zts, dst):
             for c0 in range(0, BLOCKS, 2):
-                g = take("back", back_banks, "g")
+                moved = take("back", BACK_BANKS)
                 for u in range(2):
                     for cc in range(2):
                         s0 = (u * 2 + cc) * P
-                        nc.tensor.transpose(g[:, s0 : s0 + P], words(zts[u], c0 + cc), ident[:])
+                        nc.tensor.transpose(moved[:, s0 : s0 + P], words(zts[u], c0 + cc), ident[:])
                 nc.scalar.copy(
-                    dst[:, c0 * 4 * P : (c0 + 2) * 4 * P].bitcast(F32).rearrange("p (m u) -> p m u", u=2),
-                    g[:].rearrange("p (u m) -> p m u", u=2),
+                    dst[:, c0 * PACK * P : (c0 + 2) * PACK * P].bitcast(F32).rearrange("p (m u) -> p m u", u=2),
+                    moved[:].rearrange("p (u m) -> p m u", u=2),
                 )
 
         def back_one(zt, dst, u):
             for c0 in range(0, BLOCKS, 4):
-                g = take("back", back_banks, "g")
+                moved = take("back", BACK_BANKS)
                 for cc in range(4):
-                    nc.tensor.transpose(g[:, cc * P : (cc + 1) * P], words(zt, c0 + cc), ident[:])
+                    nc.tensor.transpose(moved[:, cc * P : (cc + 1) * P], words(zt, c0 + cc), ident[:])
                 w0 = u * T2 + c0 * P
-                nc.scalar.copy(dst[:, 2 * w0 : 2 * (w0 + BANK)].bitcast(F32), g[:])
+                nc.scalar.copy(dst[:, 2 * w0 : 2 * (w0 + BANK)].bitcast(F32), moved[:])
 
-        w2_raw = sb("w2_raw", PASSES * 4 * N, F32, tag="w2_raw")
+        w2_raw = sb("w2_raw", PASSES * PACK * N, F32, tag="w2_raw")
         nc.sync.dma_start(
             w2_raw[:].rearrange("p (b x) -> p b x", b=PASSES),
-            w2.rearrange("(b p j) n -> p b (j n)", b=PASSES, j=4),
+            w2.rearrange("(b p j) n -> p b (j n)", b=PASSES, j=PACK),
         )
-
         load_kept(0)
         load_kept(1)
+
         weigh(0)
         weigh(1)
-        features(0, [0, 1])
-        features(1, [0, 1])
+        features(0, SUM_BANKS[:1] + FEATURE_BANKS)
+        features(1, FEATURE_BANKS)
         for k in range(2, TILES):
             weigh(k)
-        features(2, [0, 1])
-        features(3, [0, 1])
+        features(2, FEATURE_BANKS)
+        features(3, FEATURE_BANKS)
         scatter(0)
         scatter(1)
 
-        w2_bf = sb("w2_bf", PASSES * 4 * N, BF16, tag="zt1")
+        w2_bf = sb("w2_bf", PASSES * PACK * N, BF16, tag="zt1")
         w2_codes = sb("w2_codes", PASSES * N, U32)
         w2_sc = sb("w2_sc", PASSES * N, U8)
         for b in range(PASSES):
-            cols = slice(b * 4 * N, (b + 1) * 4 * N)
+            cols = slice(b * PACK * N, (b + 1) * PACK * N)
             nc.scalar.copy(
-                w2_bf[:, cols].rearrange("p (t m j) -> p m j t", t=4, j=4),
-                w2_raw[:, cols].rearrange("p (j m t) -> p m j t", t=4, j=4),
+                w2_bf[:, cols].rearrange("p (t m j) -> p m j t", t=PACK, j=PACK),
+                w2_raw[:, cols].rearrange("p (j m t) -> p m j t", t=PACK, j=PACK),
             )
         nc.vector.quantize_mx(out=w2_codes[:].bitcast(FP8X4), scales=w2_sc[:], in_=w2_bf[:])
 
         zt = [sb("zt%d" % u, BLOCKS * 2 * P, BF16, tag="zt%d" % u) for u in range(2)]
-        z0 = sb("z0", 4 * T2, BF16)
-        z1_words = sb("z1_words", 4 * T2, BF16)
+        z0 = sb("z0", PACK * T2, BF16)
+        z1_words = sb("z1_words", PACK * T2, BF16)
 
-        features(4, [0, 1])
-        features(5, [0, 1])
+        features(4, FEATURE_BANKS)
+        features(5, FEATURE_BANKS)
         blend_pair(0, zt[0])
         load_kept(2)
         scatter(2)
         scatter(3)
-        features(6, [fwd_banks[0], fwd_banks[1]])
-        features(7, [fwd_banks[2], fwd_banks[0]])
+        features(6, [SUM_BANKS[0], SUM_BANKS[1]])
+        features(7, [SUM_BANKS[2], SUM_BANKS[0]])
         blend_pair(1, zt[1])
         load_kept(3)
         back_both(zt, z0)
@@ -283,7 +292,7 @@ def tile_list_berth_page_nowcast_kernel(
         blend_pair(2, zt[0])
         back_one(zt[0], z1_words, 0)
         scatter(6)
-        blend_single(6, zt[1])
+        blend_low(6, zt[1])
         back_one(zt[1], z1_words, 1)
         scatter(7)
 
@@ -291,12 +300,13 @@ def tile_list_berth_page_nowcast_kernel(
         z0_sc = sb("z0_sc", T2, U8)
         y_codes = sb("y_codes", T2, U32)
         y_sc = sb("y_sc", T2, U8)
-        y_rows = out_0.rearrange("(p t) m -> p t m", t=4)
+        y_rows = out_0.rearrange("(p t) m -> p t m", t=PACK)
         y_words = out_1[0].rearrange("p m t -> p (m t)").bitcast(I32)
         last = TILES - 1
-        z1_ring = sb("z1_ring", 2 * 4 * BANK, BF16, tag="zt1")
+        z1_ring = sb("z1_ring", 2 * PACK * BANK, BF16, tag="zt1")
         for j in range(CHUNKS):
             cols = slice(j * BANK, (j + 1) * BANK)
+            final = j == CHUNKS - 1
             w0 = T2 + j * BANK
             nc.vector.tensor_tensor(
                 z1_words[:, 2 * w0 : 2 * (w0 + BANK)].rearrange("p (m e) -> p m e", e=2)[:, :, 1],
@@ -304,20 +314,22 @@ def tile_list_berth_page_nowcast_kernel(
                 kept_sb[last // 2][:, w0 : w0 + BANK],
                 ALU.add,
             )
-            z1 = z1_ring[:, (j % 2) * 4 * BANK : (j % 2 + 1) * 4 * BANK]
+            z1 = z1_ring[:, (j % 2) * PACK * BANK : (j % 2 + 1) * PACK * BANK]
             nc.scalar.copy(
                 z1.bitcast(F32).rearrange("p (m u) -> p m u", u=2),
                 z1_words[:].bitcast(F32).rearrange("p (u m) -> p m u", u=2)[:, cols, :],
             )
             nc.vector.quantize_mx(
-                out=z0_codes[:, cols].bitcast(FP8X4), scales=z0_sc[:, cols], in_=z0[:, 4 * j * BANK : 4 * (j + 1) * BANK]
+                out=z0_codes[:, cols].bitcast(FP8X4),
+                scales=z0_sc[:, cols],
+                in_=z0[:, PACK * j * BANK : PACK * (j + 1) * BANK],
             )
-            z1_codes = sb("z1_codes%d" % j, BANK, U32, tag="z1c", bufs=2)
-            z1_sc = sb("z1_sc%d" % j, BANK, U8, tag="z1s", bufs=2)
+            z1_codes = sb("z1_codes%d" % j, BANK, U32, tag="z1_codes", bufs=2)
+            z1_sc = sb("z1_sc%d" % j, BANK, U8, tag="z1_sc", bufs=2)
             nc.vector.quantize_mx(out=z1_codes[:].bitcast(FP8X4), scales=z1_sc[:], in_=z1)
-            y = sb("y%d" % j, 4 * BANK, F32, tag="rw", bufs=4)
-            for t in range(4):
-                acc = bank(4 * (j % 2) + t, "y%d_%d" % (j, t))
+            y = sb("y%d" % j, PACK * BANK, F32, tag="rw", bufs=4)
+            for t in range(PACK):
+                acc = bank(PACK * (j % 2) + t, "y%d_%d" % (j, t))
                 moving = [(z1_codes[:], z1_sc[:], 1), (z0_codes[:, cols], z0_sc[:, cols], 0)]
                 for i, (codes, scales, b) in enumerate(moving):
                     c0 = b * N + t * P
@@ -331,26 +343,26 @@ def tile_list_berth_page_nowcast_kernel(
                         stop=(i == PASSES - 1),
                     )
                 y_t = y[:, t * BANK : (t + 1) * BANK]
-                if t % 2 == 0 and j < CHUNKS - 1:
+                if t % 2 == 0 and not final:
                     raw = sb("raw%d_%d" % (j, t), BANK, F32, tag="raw", bufs=2)
                     nc.scalar.copy(raw[:], acc[:])
                     nc.vector.tensor_scalar_max(y_t, raw[:], floor_sb[:, t : t + 1])
                 else:
                     nc.vector.tensor_scalar_max(y_t, acc[:], floor_sb[:, t : t + 1])
-                if j == CHUNKS - 1:
+                if final:
                     nc.sync.dma_start(y_rows[:, t, cols], y_t)
-            if j < CHUNKS - 1:
-                nc.sync.dma_start(y_rows[:, :, cols], y[:].rearrange("p (t m) -> p t m", t=4))
-            y_bf = sb("y_bf%d" % j, 4 * BANK, BF16, tag="h", bufs=4)
-            rounded = y_bf[:].rearrange("p (c i t) -> p c t i", t=4, i=4)
-            by_column = y[:].rearrange("p (t c i) -> p c t i", t=4, i=4)
-            if j < CHUNKS - 1:
-                nc.scalar.copy(rounded, by_column)
+            if not final:
+                nc.sync.dma_start(y_rows[:, :, cols], y[:].rearrange("p (t m) -> p t m", t=PACK))
+            y_bf = sb("y_bf%d" % j, PACK * BANK, BF16, tag="h", bufs=4)
+            rounded = y_bf[:].rearrange("p (c i t) -> p c t i", t=PACK, i=4)
+            by_column = y[:].rearrange("p (t c i) -> p c t i", t=PACK, i=4)
+            if final:
+                nc.scalar.copy(rounded[:, :SCALAR_RUNS], by_column[:, :SCALAR_RUNS])
+                nc.vector.tensor_copy(rounded[:, SCALAR_RUNS:], by_column[:, SCALAR_RUNS:])
             else:
-                nc.scalar.copy(rounded[:, :SHARE], by_column[:, :SHARE])
-                nc.vector.tensor_copy(rounded[:, SHARE:], by_column[:, SHARE:])
+                nc.scalar.copy(rounded, by_column)
             nc.vector.quantize_mx(out=y_codes[:, cols].bitcast(FP8X4), scales=y_sc[:, cols], in_=y_bf[:])
             nc.sync.dma_start(y_words[:, cols], y_codes[:, cols].bitcast(I32))
-        for q in range(4):
+        for q in range(QUADS):
             queue = nc.sync if q % 2 == 0 else nc.scalar
             queue.dma_start(out_2[0, 4 * q : 4 * q + 4, :].bitcast(I32), y_sc[32 * q : 32 * q + 4, :].bitcast(I32))

@@ -29,7 +29,9 @@ GROUP = 16
 QUADS = 4
 ALIGN = 64
 FIRST_PIECES = [(0, 128), (128, 512), (512, 1024)]
-SCALAR_RUNS = 44
+PARTS = [(0, 512, (0, 2)), (512, 512, (0, 2)), (1024, 512, (0, 2)), (1536, 256, ()), (1792, 256, ())]
+ROUND_RUNS = 64
+STORE_COLUMNS = 1024
 FEATURE_BANKS = [0, 1]
 SUM_BANKS = [2, 3, 4]
 BACK_BANKS = [5, 6, 7]
@@ -59,42 +61,48 @@ def tile_list_berth_page_nowcast_kernel(
         one = sb("one", 1, F32)
         unit = sb("unit", 1, F32)
         ident = sb("ident", P, F32)
-        tab_sc = sb("tab_sc", T, U8, tag="w2_raw")
-        wgs_sb = sb("wgs_sb", S, F32, tag="sq", bufs=2)
-        w1_raw = sb("w1_raw", PASSES * 2 * H, U8, tag="page0")
-        w1_sc_raw = sb("w1_sc_raw", PASSES * H, U8, tag="page1")
-        v_sc1 = sb("v_sc1", S, U8)
+        tab_sc = sb("tab_sc", PASSES * T, U8, tag="w2_raw")
+        wgs_sb = sb("wgs_sb", S, F32, tag="zt1")
+        w1_raw = sb("w1_raw", PASSES * 2 * H, U8, tag="zt0")
+        w1_sc_raw = sb("w1_sc_raw", PASSES * H, U8, tag="page2")
 
         nc.vector.memset(tab_sc[:].bitcast(I32), 0)
-        nc.vector.memset(w1_sc_raw[:].bitcast(I32), 0)
         nc.vector.memset(one[:], 1.0)
-        nc.vector.memset(v_sc1[:].bitcast(I32), 0)
+        nc.vector.memset(w1_sc_raw[:].bitcast(I32), 0)
 
         nc.sync.dma_start(list1[:], offs)
-        nc.sync.dma_start(list2[:], offs2)
+        nc.scalar.dma_start(
+            rate_sb[:].rearrange("p (b t) -> p b t", b=PASSES), rate.rearrange("(b p t) -> p b t", b=PASSES, t=PACK)
+        )
         nc.sync.dma_start(
             w1_raw[:].bitcast(I32).rearrange("p (a c) -> p a c", a=PASSES),
             w1_words.bitcast(I32).rearrange("a p c -> p a c"),
         )
-        for q in range(QUADS):
-            nc.sync.dma_start(
-                tab_sc[32 * q : 32 * q + 8, :].bitcast(I32), tab_scales[:, 4 * q : 4 * q + 4, :].bitcast(I32)
-            )
-        for q in range(QUADS):
-            nc.scalar.dma_start(
-                w1_sc_raw[32 * q : 32 * q + 4, :].bitcast(I32).rearrange("r (a c) -> r a c", a=PASSES),
-                w1_scales[:, 4 * q : 4 * q + 4, :].bitcast(I32).rearrange("a r c -> r a c"),
-            )
-        nc.sync.dma_start(wgs_sb[:], wgs)
+
+        def load_scales(plane, scales):
+            for q in range(QUADS):
+                nc.sync.dma_start(
+                    plane[32 * q : 32 * q + 4, :].bitcast(I32).rearrange("r (a c) -> r a c", a=PASSES),
+                    scales[:, 4 * q : 4 * q + 4, :].bitcast(I32).rearrange("a r c -> r a c"),
+                )
+
         tab = [sb("tab%d" % a, T, I32, tag="big%d" % a) for a in range(PASSES)]
-        for a in range(PASSES):
+
+        def load_table(a):
             nc.sync.dma_start(tab[a][:], tab_words[a].rearrange("p c i -> p (c i)").bitcast(I32))
-        nc.scalar.dma_start(
-            rate_sb[:].rearrange("p (b t) -> p b t", b=PASSES), rate.rearrange("(b p t) -> p b t", b=PASSES, t=PACK)
-        )
+
+        load_scales(tab_sc, tab_scales)
+        nc.sync.dma_start(wgs_sb[:], wgs)
+        load_table(0)
+        load_scales(w1_sc_raw, w1_scales)
+        load_table(1)
+        nc.sync.dma_start(list2[:], offs2)
 
         make_identity(nc, ident[:])
         nc.scalar.activation(unit[:], one[:], ACT.Sqrt)
+
+        pages = [sb("page0", T2, F32, tag="page0")]
+        nc.vector.memset(pages[0][:], 0.0)
 
         w1_codes = sb("w1_codes", PASSES * 2 * H, U8)
         w1_sc = sb("w1_sc", PASSES * H, U8)
@@ -103,26 +111,26 @@ def tile_list_berth_page_nowcast_kernel(
             w1_raw[:].bitcast(U16).rearrange("p (g m t) -> p g t m", t=PACK, m=P),
         )
 
-        v_sc0 = sb("v_sc0", S, U8)
-        nc.vector.tensor_copy(v_sc0[:], tab_sc[:].indirect(list1[:]))
-        for i in range(4):
-            nc.sync.dma_start(v_sc1[i:P:32, :].bitcast(I32), v_sc0[4 + i : P : 32, :].bitcast(I32))
-        v_sc = [v_sc0, v_sc1]
+        v_sc = [sb("v_sc%d" % a, S, U8) for a in range(PASSES)]
+        for a in range(PASSES):
+            nc.vector.tensor_copy(v_sc[a][:], tab_sc[:, a * T : (a + 1) * T].indirect(list1[:]))
+        v_codes = []
+
+        def gather_words(a):
+            halves = []
+            for i in range(S // BANK):
+                half = sb("v_codes%d_%d" % (a, i), BANK, U32, tag="strip%d" % (2 * a + i))
+                offsets = list1[:, i * BANK // GROUP : (i + 1) * BANK // GROUP]
+                nc.vector.tensor_copy(half[:], tab[a][:].bitcast(U32).indirect(offsets))
+                halves.append(half)
+            v_codes.append(halves)
+
+        gather_words(0)
         nc.vector.tensor_copy(
             w1_sc[:].rearrange("p (g t m) -> p g t m", t=PACK, m=P),
             w1_sc_raw[:].rearrange("p (g m t) -> p g t m", t=PACK, m=P),
         )
-        nc.gpsimd.dma_start(floor_sb[:], floor.rearrange("(p t) -> p t", t=PACK))
-        v_codes = [sb("v_codes%d" % a, S, U32) for a in range(PASSES)]
-        nc.vector.tensor_copy(v_codes[0][:], tab[0][:].bitcast(U32).indirect(list1[:]))
-        for lo in range(0, S, BANK):
-            nc.vector.tensor_copy(
-                v_codes[1][:, lo : lo + BANK],
-                tab[1][:].bitcast(U32).indirect(list1[:, lo // GROUP : (lo + BANK) // GROUP]),
-            )
-
-        pages = [sb("page0", T2, F32, tag="page0")]
-        nc.vector.memset(pages[0][:], 0.0)
+        gather_words(1)
 
         rw = [sb("rw%d" % i, 2 * S, F32, tag="rw", bufs=4) for i in range(TILES // 2)]
 
@@ -131,24 +139,21 @@ def tile_list_berth_page_nowcast_kernel(
                 rw[k // 2][:, (k % 2) * S : (k % 2 + 1) * S], wgs_sb[:], ACT.Copy, scale=rate_sb[:, k : k + 1]
             )
 
-        kept_rows = kept.rearrange("(b p u e) m -> b u p (e m)", b=PASSES, u=2, e=2)
+        kept_rows = kept.rearrange("(b p u e) m -> b u p e m", b=PASSES, u=2, e=2)
         kept_sb = {}
 
-        def load_kept(pair):
-            kept_sb[pair] = sb("kept%d" % pair, 2 * T2, F32, tag="big%d" % (pair % 2))
-            nc.sync.dma_start(kept_sb[pair][:], kept_rows[pair // 2, pair % 2])
+        def load_kept(pair, rows):
+            kept_sb[pair] = sb("kept%d" % pair, rows * T2, F32, tag="big%d" % (pair % 2))
+            nc.sync.dma_start(
+                kept_sb[pair][:].rearrange("p (e m) -> p e m", e=rows), kept_rows[pair // 2, pair % 2][:, :rows, :]
+            )
 
         h = {}
 
         def features(k, banks):
             b, t = divmod(k, PACK)
-            if k < PAGES - 1:
-                sq = sb("sq%d" % k, S, F32, tag="page%d" % (k + 1))
-            elif k == PAGES - 1:
-                sq = sb("sq%d" % k, S, F32, tag="zt1")
-            else:
-                sq = sb("sq%d" % k, S, F32, tag="sq", bufs=2)
-            h[k] = sb("h%d" % k, S, F32, tag="h", bufs=4)
+            h[k] = sb("h%d" % k, S, F32, tag="h", bufs=TILES)
+            sq = sb("sq%d" % k, S, F32, tag="page%d" % (k + 1)) if k < 2 else h[k]
             spans = FIRST_PIECES if k == 0 else [(0, BANK), (BANK, S)]
             for i, (lo, hi) in enumerate(spans):
                 acc = bank(banks[i], "a%d_%d" % (k, i))
@@ -160,7 +165,7 @@ def tile_list_berth_page_nowcast_kernel(
                             out=acc[:, n0 - lo : n0 - lo + width],
                             lhsT=w1_codes[:, 2 * c0 : 2 * (c0 + P)].bitcast(FP4X4),
                             lhsT_scale=w1_sc[:, c0 : c0 + P],
-                            rhs=v_codes[a][:, n0 : n0 + width].bitcast(FP8X4),
+                            rhs=v_codes[a][n0 // BANK][:, n0 % BANK : n0 % BANK + width].bitcast(FP8X4),
                             rhs_scale=v_sc[a][:, n0 : n0 + width],
                             start=(a == 0),
                             stop=(a == PASSES - 1),
@@ -169,8 +174,9 @@ def tile_list_berth_page_nowcast_kernel(
                 if k == 0:
                     nc.scalar.activation(h[k][:, lo:hi], sq[:, lo:hi], ACT.Sqrt, bias=unit[:])
             if k > 0:
-                nc.scalar.activation(h[k][:], sq[:], ACT.Sqrt, bias=unit[:])
-            if k < PAGES - 1:
+                for lo, hi in spans:
+                    nc.scalar.activation(h[k][:, lo:hi], sq[:, lo:hi], ACT.Sqrt, bias=unit[:])
+            if k < 2:
                 pages.append(sb("page%d" % (k + 1), T2, F32, tag="page%d" % (k + 1)))
                 nc.gpsimd.memset(pages[k + 1][:], 0.0)
 
@@ -247,19 +253,17 @@ def tile_list_berth_page_nowcast_kernel(
             w2_raw[:].rearrange("p (b x) -> p b x", b=PASSES),
             w2.rearrange("(b p j) n -> p b (j n)", b=PASSES, j=PACK),
         )
-        load_kept(0)
-        load_kept(1)
+        load_kept(0, 2)
+        load_kept(1, 2)
+        nc.sync.dma_start(floor_sb[:], floor.rearrange("(p t) -> p t", t=PACK))
 
-        weigh(0)
-        weigh(1)
-        features(0, SUM_BANKS[:1] + FEATURE_BANKS)
-        features(1, FEATURE_BANKS)
-        for k in range(2, TILES):
+        for k in range(TILES):
             weigh(k)
-        features(2, FEATURE_BANKS)
-        features(3, FEATURE_BANKS)
-        scatter(0)
-        scatter(1)
+        features(0, SUM_BANKS[:1] + FEATURE_BANKS)
+        for k in range(1, 4):
+            features(k, FEATURE_BANKS)
+        for k in range(3):
+            scatter(k)
 
         w2_bf = sb("w2_bf", PASSES * PACK * N, BF16, tag="zt1")
         w2_codes = sb("w2_codes", PASSES * N, U32)
@@ -271,21 +275,26 @@ def tile_list_berth_page_nowcast_kernel(
                 w2_raw[:, cols].rearrange("p (j m t) -> p m j t", t=PACK, j=PACK),
             )
         nc.vector.quantize_mx(out=w2_codes[:].bitcast(FP8X4), scales=w2_sc[:], in_=w2_bf[:])
+        pages.append(sb("page3", T2, F32, tag="w2_raw"))
+        nc.gpsimd.memset(pages[3][:], 0.0)
+        scatter(3)
 
         zt = [sb("zt%d" % u, BLOCKS * 2 * P, BF16, tag="zt%d" % u) for u in range(2)]
         z0 = sb("z0", PACK * T2, BF16)
         z1_words = sb("z1_words", PACK * T2, BF16)
 
         features(4, FEATURE_BANKS)
-        features(5, FEATURE_BANKS)
         blend_pair(0, zt[0])
-        load_kept(2)
-        scatter(2)
-        scatter(3)
-        features(6, [SUM_BANKS[0], SUM_BANKS[1]])
-        features(7, [SUM_BANKS[2], SUM_BANKS[0]])
+        load_kept(2, 2)
+        for k in range(5, TILES):
+            features(k, FEATURE_BANKS)
+        last = TILES - 1
+        kept_last = []
+        for j in range(CHUNKS):
+            kept_last.append(sb("kept_last%d" % j, BANK, F32, tag="strip%d" % j))
+            nc.sync.dma_start(kept_last[j][:], kept_rows[1, 1][:, 1, j * BANK : (j + 1) * BANK])
         blend_pair(1, zt[1])
-        load_kept(3)
+        load_kept(3, 1)
         back_both(zt, z0)
         scatter(4)
         scatter(5)
@@ -296,73 +305,111 @@ def tile_list_berth_page_nowcast_kernel(
         back_one(zt[1], z1_words, 1)
         scatter(7)
 
-        z0_codes = sb("z0_codes", T2, U32)
         z0_sc = sb("z0_sc", T2, U8)
+        z1_codes = sb("z1_codes", T2, U32, tag="page0")
+        z1_sc = sb("z1_sc", T2, U8)
         y_codes = sb("y_codes", T2, U32)
         y_sc = sb("y_sc", T2, U8)
         y_rows = out_0.rearrange("(p t) m -> p t m", t=PACK)
         y_words = out_1[0].rearrange("p m t -> p (m t)").bitcast(I32)
-        last = TILES - 1
-        z1_ring = sb("z1_ring", 2 * PACK * BANK, BF16, tag="zt1")
-        for j in range(CHUNKS):
-            cols = slice(j * BANK, (j + 1) * BANK)
-            final = j == CHUNKS - 1
+        z0_codes, z1, y, y_bf = {}, {}, {}, {}
+
+        def span(j):
+            return slice(j * BANK, (j + 1) * BANK)
+
+        def finish_z(j):
             w0 = T2 + j * BANK
             nc.vector.tensor_tensor(
                 z1_words[:, 2 * w0 : 2 * (w0 + BANK)].rearrange("p (m e) -> p m e", e=2)[:, :, 1],
-                pages[last % PAGES][:, cols],
-                kept_sb[last // 2][:, w0 : w0 + BANK],
+                pages[last % PAGES][:, span(j)],
+                kept_last[j][:],
                 ALU.add,
             )
-            z1 = z1_ring[:, (j % 2) * PACK * BANK : (j % 2 + 1) * PACK * BANK]
+            z1[j] = sb("z1_%d" % j, PACK * BANK, BF16, tag="h", bufs=TILES)
             nc.scalar.copy(
-                z1.bitcast(F32).rearrange("p (m u) -> p m u", u=2),
-                z1_words[:].bitcast(F32).rearrange("p (u m) -> p m u", u=2)[:, cols, :],
+                z1[j][:].bitcast(F32).rearrange("p (m u) -> p m u", u=2),
+                z1_words[:].bitcast(F32).rearrange("p (u m) -> p m u", u=2)[:, span(j), :],
             )
+
+        def quantise_z(j):
+            z0_codes[j] = sb("z0_codes%d" % j, BANK, U32, tag="strip%d" % j)
             nc.vector.quantize_mx(
-                out=z0_codes[:, cols].bitcast(FP8X4),
-                scales=z0_sc[:, cols],
+                out=z0_codes[j][:].bitcast(FP8X4),
+                scales=z0_sc[:, span(j)],
                 in_=z0[:, PACK * j * BANK : PACK * (j + 1) * BANK],
             )
-            z1_codes = sb("z1_codes%d" % j, BANK, U32, tag="z1_codes", bufs=2)
-            z1_sc = sb("z1_sc%d" % j, BANK, U8, tag="z1_sc", bufs=2)
-            nc.vector.quantize_mx(out=z1_codes[:].bitcast(FP8X4), scales=z1_sc[:], in_=z1)
-            y = sb("y%d" % j, PACK * BANK, F32, tag="rw", bufs=4)
-            for t in range(PACK):
-                acc = bank(PACK * (j % 2) + t, "y%d_%d" % (j, t))
-                moving = [(z1_codes[:], z1_sc[:], 1), (z0_codes[:, cols], z0_sc[:, cols], 0)]
-                for i, (codes, scales, b) in enumerate(moving):
+            nc.vector.quantize_mx(out=z1_codes[:, span(j)].bitcast(FP8X4), scales=z1_sc[:, span(j)], in_=z1[j][:])
+
+        def scores(i):
+            lo, width, by_scalar = PARTS[i]
+            j, cols = lo // BANK, slice(lo, lo + width)
+            y[i] = sb("y%d" % i, PACK * width, F32, tag="rw", bufs=4)
+            acc = [bank(PACK * (i % 2) + t, "y%d_%d" % (i, t)) for t in range(PACK)]
+            moving = [
+                (z0_codes[j][:, lo % BANK : lo % BANK + width], z0_sc[:, cols]),
+                (z1_codes[:, cols], z1_sc[:, cols]),
+            ]
+            for b, (codes, scales) in enumerate(moving):
+                for t in range(PACK):
                     c0 = b * N + t * P
                     nc.tensor.matmul_mx(
-                        out=acc[:],
+                        out=acc[t][:, :width],
                         lhsT=w2_codes[:, c0 : c0 + P].bitcast(FP8X4),
                         lhsT_scale=w2_sc[:, c0 : c0 + P],
                         rhs=codes.bitcast(FP8X4),
                         rhs_scale=scales,
-                        start=(i == 0),
-                        stop=(i == PASSES - 1),
+                        start=(b == 0),
+                        stop=(b == PASSES - 1),
                     )
-                y_t = y[:, t * BANK : (t + 1) * BANK]
-                if t % 2 == 0 and not final:
-                    raw = sb("raw%d_%d" % (j, t), BANK, F32, tag="raw", bufs=2)
-                    nc.scalar.copy(raw[:], acc[:])
-                    nc.vector.tensor_scalar_max(y_t, raw[:], floor_sb[:, t : t + 1])
+            rows = STORE_COLUMNS // width
+            for t in range(PACK):
+                y_t = y[i][:, t * width : (t + 1) * width]
+                if t in by_scalar:
+                    nc.scalar.copy(y_t, acc[t][:, :width])
+                    nc.vector.tensor_scalar_max(y_t, y_t, floor_sb[:, t : t + 1])
                 else:
-                    nc.vector.tensor_scalar_max(y_t, acc[:], floor_sb[:, t : t + 1])
-                if final:
-                    nc.sync.dma_start(y_rows[:, t, cols], y_t)
-            if not final:
-                nc.sync.dma_start(y_rows[:, :, cols], y[:].rearrange("p (t m) -> p t m", t=PACK))
-            y_bf = sb("y_bf%d" % j, PACK * BANK, BF16, tag="h", bufs=4)
-            rounded = y_bf[:].rearrange("p (c i t) -> p c t i", t=PACK, i=4)
-            by_column = y[:].rearrange("p (t c i) -> p c t i", t=PACK, i=4)
-            if final:
-                nc.scalar.copy(rounded[:, :SCALAR_RUNS], by_column[:, :SCALAR_RUNS])
-                nc.vector.tensor_copy(rounded[:, SCALAR_RUNS:], by_column[:, SCALAR_RUNS:])
+                    nc.vector.tensor_scalar_max(y_t, acc[t][:, :width], floor_sb[:, t : t + 1])
+                if (t + 1) % rows == 0:
+                    nc.sync.dma_start(
+                        y_rows[:, t + 1 - rows : t + 1, cols],
+                        y[i][:, (t + 1 - rows) * width : (t + 1) * width].rearrange("p (t m) -> p t m", t=rows),
+                    )
+
+        def round_y(i):
+            width = PARTS[i][1]
+            y_bf[i] = sb("y_bf%d" % i, PACK * width, BF16, tag="h", bufs=TILES)
+            rounded = y_bf[i][:].rearrange("p (c i t) -> p c t i", t=PACK, i=4)
+            by_column = y[i][:].rearrange("p (t c i) -> p c t i", t=PACK, i=4)
+            if i == len(PARTS) - 1:
+                nc.vector.tensor_copy(rounded, by_column)
             else:
-                nc.scalar.copy(rounded, by_column)
-            nc.vector.quantize_mx(out=y_codes[:, cols].bitcast(FP8X4), scales=y_sc[:, cols], in_=y_bf[:])
+                for c0 in range(0, width // 4, ROUND_RUNS):
+                    nc.scalar.copy(rounded[:, c0 : c0 + ROUND_RUNS], by_column[:, c0 : c0 + ROUND_RUNS])
+
+        def planes(i):
+            lo, width, by_scalar = PARTS[i]
+            cols = slice(lo, lo + width)
+            nc.vector.quantize_mx(out=y_codes[:, cols].bitcast(FP8X4), scales=y_sc[:, cols], in_=y_bf[i][:])
             nc.sync.dma_start(y_words[:, cols], y_codes[:, cols].bitcast(I32))
+
+        finish_z(0)
+        finish_z(1)
+        quantise_z(0)
+        finish_z(2)
+        finish_z(3)
+        quantise_z(1)
+        scores(0)
+        quantise_z(2)
+        scores(1)
+        round_y(0)
+        quantise_z(3)
+        for i in range(2, len(PARTS)):
+            scores(i)
+            planes(i - 2)
+            round_y(i - 1)
+        round_y(len(PARTS) - 1)
+        planes(len(PARTS) - 2)
+        planes(len(PARTS) - 1)
         for q in range(QUADS):
             queue = nc.sync if q % 2 == 0 else nc.scalar
             queue.dma_start(out_2[0, 4 * q : 4 * q + 4, :].bitcast(I32), y_sc[32 * q : 32 * q + 4, :].bitcast(I32))

@@ -32,6 +32,7 @@ FIRST_PIECES = [(0, 128), (128, 512), (512, 1024)]
 PARTS = [(0, 512, (0, 2)), (512, 512, (0, 2)), (1024, 512, (0, 2)), (1536, 256, ()), (1792, 256, ())]
 ROUND_RUNS = 64
 STORE_COLUMNS = 1024
+VECTOR_WEIGHS = 4
 FEATURE_BANKS = [0, 1]
 SUM_BANKS = [2, 3, 4]
 BACK_BANKS = [5, 6, 7]
@@ -61,59 +62,63 @@ def tile_list_berth_page_nowcast_kernel(
         one = sb("one", 1, F32)
         unit = sb("unit", 1, F32)
         ident = sb("ident", P, F32)
-        tab_sc = sb("tab_sc", PASSES * T, U8, tag="w2_raw")
+        tab_sc = sb("tab_sc", T, U8, tag="page1")
         wgs_sb = sb("wgs_sb", S, F32, tag="zt1")
-        w1_raw = sb("w1_raw", PASSES * 2 * H, U8, tag="zt0")
-        w1_sc_raw = sb("w1_sc_raw", PASSES * H, U8, tag="page2")
+        w1_raw = sb("w1_raw", PASSES * 2 * H, U8, tag="w2_raw")
+        w1_sc_raw = sb("w1_sc_raw", H, U8, tag="page2")
+        planes1 = [sb("planes1_%d" % a, S + H, U8) for a in range(PASSES)]
 
-        nc.vector.memset(tab_sc[:].bitcast(I32), 0)
+        nc.gpsimd.memset(tab_sc[:].bitcast(I32), 0)
         nc.vector.memset(one[:], 1.0)
-        nc.vector.memset(w1_sc_raw[:].bitcast(I32), 0)
+        nc.gpsimd.memset(w1_sc_raw[:].bitcast(I32), 0)
+
+        nc.gpsimd.memset(planes1[1][:].bitcast(I32), 0)
 
         nc.sync.dma_start(list1[:], offs)
         nc.scalar.dma_start(
             rate_sb[:].rearrange("p (b t) -> p b t", b=PASSES), rate.rearrange("(b p t) -> p b t", b=PASSES, t=PACK)
         )
+        nc.sync.dma_start(list2[:], offs2)
+        for rows, scales in [(tab_sc, tab_scales), (w1_sc_raw, w1_scales)]:
+            for a in range(PASSES):
+                nc.sync.dma_start(rows[4 * a : P : 8, :].bitcast(I32), scales[a].bitcast(I32))
         nc.sync.dma_start(
             w1_raw[:].bitcast(I32).rearrange("p (a c) -> p a c", a=PASSES),
             w1_words.bitcast(I32).rearrange("a p c -> p a c"),
         )
-
-        def load_scales(plane, scales):
-            for q in range(QUADS):
-                nc.sync.dma_start(
-                    plane[32 * q : 32 * q + 4, :].bitcast(I32).rearrange("r (a c) -> r a c", a=PASSES),
-                    scales[:, 4 * q : 4 * q + 4, :].bitcast(I32).rearrange("a r c -> r a c"),
-                )
-
+        nc.sync.dma_start(wgs_sb[:], wgs)
         tab = [sb("tab%d" % a, T, I32, tag="big%d" % a) for a in range(PASSES)]
 
         def load_table(a):
             nc.sync.dma_start(tab[a][:], tab_words[a].rearrange("p c i -> p (c i)").bitcast(I32))
 
-        load_scales(tab_sc, tab_scales)
-        nc.sync.dma_start(wgs_sb[:], wgs)
         load_table(0)
-        load_scales(w1_sc_raw, w1_scales)
         load_table(1)
-        nc.sync.dma_start(list2[:], offs2)
+
+        staged = planes1[0]
+        v_rows = sb("v_rows", S, U8)
+        nc.vector.tensor_copy(v_rows[:], tab_sc[:].indirect(list1[:]))
+        nc.vector.tensor_copy(
+            staged[:, S:].rearrange("p (b t m) -> p b t m", t=PACK, m=P),
+            w1_sc_raw[:].rearrange("p (b m t) -> p b t m", t=PACK, m=P),
+        )
+        nc.vector.tensor_copy(staged[:, :S].bitcast(I32), v_rows[:].bitcast(I32))
+        for a in range(PASSES):
+            for i in range(1 - a, 4):
+                nc.scalar.dma_start(planes1[a][i:P:32, :].bitcast(I32), staged[8 * i + 4 * a : P : 32, :].bitcast(I32))
+
+        pages = [sb("page0", T2, F32, tag="page0")]
+        nc.gpsimd.memset(pages[0][:], 0.0)
 
         make_identity(nc, ident[:])
         nc.scalar.activation(unit[:], one[:], ACT.Sqrt)
 
-        pages = [sb("page0", T2, F32, tag="page0")]
-        nc.vector.memset(pages[0][:], 0.0)
-
         w1_codes = sb("w1_codes", PASSES * 2 * H, U8)
-        w1_sc = sb("w1_sc", PASSES * H, U8)
         nc.vector.tensor_copy(
             w1_codes[:].bitcast(U16).rearrange("p (g t m) -> p g t m", t=PACK, m=P),
             w1_raw[:].bitcast(U16).rearrange("p (g m t) -> p g t m", t=PACK, m=P),
         )
 
-        v_sc = [sb("v_sc%d" % a, S, U8) for a in range(PASSES)]
-        for a in range(PASSES):
-            nc.vector.tensor_copy(v_sc[a][:], tab_sc[:, a * T : (a + 1) * T].indirect(list1[:]))
         v_codes = []
 
         def gather_words(a):
@@ -126,18 +131,16 @@ def tile_list_berth_page_nowcast_kernel(
             v_codes.append(halves)
 
         gather_words(0)
-        nc.vector.tensor_copy(
-            w1_sc[:].rearrange("p (g t m) -> p g t m", t=PACK, m=P),
-            w1_sc_raw[:].rearrange("p (g m t) -> p g t m", t=PACK, m=P),
-        )
         gather_words(1)
 
         rw = [sb("rw%d" % i, 2 * S, F32, tag="rw", bufs=4) for i in range(TILES // 2)]
 
         def weigh(k):
-            nc.scalar.activation(
-                rw[k // 2][:, (k % 2) * S : (k % 2 + 1) * S], wgs_sb[:], ACT.Copy, scale=rate_sb[:, k : k + 1]
-            )
+            rw_k = rw[k // 2][:, (k % 2) * S : (k % 2 + 1) * S]
+            if k < VECTOR_WEIGHS:
+                nc.vector.tensor_scalar_mul(rw_k, wgs_sb[:], rate_sb[:, k : k + 1])
+            else:
+                nc.scalar.activation(rw_k, wgs_sb[:], ACT.Copy, scale=rate_sb[:, k : k + 1])
 
         kept_rows = kept.rearrange("(b p u e) m -> b u p e m", b=PASSES, u=2, e=2)
         kept_sb = {}
@@ -151,7 +154,6 @@ def tile_list_berth_page_nowcast_kernel(
         h = {}
 
         def features(k, banks):
-            b, t = divmod(k, PACK)
             h[k] = sb("h%d" % k, S, F32, tag="h", bufs=TILES)
             sq = sb("sq%d" % k, S, F32, tag="page%d" % (k + 1)) if k < 2 else h[k]
             spans = FIRST_PIECES if k == 0 else [(0, BANK), (BANK, S)]
@@ -160,13 +162,13 @@ def tile_list_berth_page_nowcast_kernel(
                 width = BANK if hi - lo == BANK else P
                 for n0 in range(lo, hi, width):
                     for a in range(PASSES):
-                        c0 = a * H + b * BANK + t * P
+                        c0 = a * H + k * P
                         nc.tensor.matmul_mx(
                             out=acc[:, n0 - lo : n0 - lo + width],
                             lhsT=w1_codes[:, 2 * c0 : 2 * (c0 + P)].bitcast(FP4X4),
-                            lhsT_scale=w1_sc[:, c0 : c0 + P],
+                            lhsT_scale=planes1[a][:, S + k * P : S + (k + 1) * P],
                             rhs=v_codes[a][n0 // BANK][:, n0 % BANK : n0 % BANK + width].bitcast(FP8X4),
-                            rhs_scale=v_sc[a][:, n0 : n0 + width],
+                            rhs_scale=planes1[a][:, n0 : n0 + width],
                             start=(a == 0),
                             stop=(a == PASSES - 1),
                         )
@@ -257,11 +259,14 @@ def tile_list_berth_page_nowcast_kernel(
         load_kept(1, 2)
         nc.sync.dma_start(floor_sb[:], floor.rearrange("(p t) -> p t", t=PACK))
 
-        for k in range(TILES):
+        for k in range(VECTOR_WEIGHS):
             weigh(k)
         features(0, SUM_BANKS[:1] + FEATURE_BANKS)
-        for k in range(1, 4):
-            features(k, FEATURE_BANKS)
+        features(1, FEATURE_BANKS)
+        for k in range(VECTOR_WEIGHS, TILES):
+            weigh(k)
+        features(2, FEATURE_BANKS)
+        features(3, FEATURE_BANKS)
         for k in range(3):
             scatter(k)
 

@@ -63,8 +63,8 @@ def tile_list_berth_page_nowcast_kernel(
         unit = sb("unit", 1, F32)
         ident = sb("ident", P, F32)
         tab_sc = sb("tab_sc", T, U8, tag="page1")
-        wgs_sb = sb("wgs_sb", S, F32, tag="zt1")
-        w1_raw = sb("w1_raw", PASSES * 2 * H, U8, tag="w2_raw")
+        wgs_sb = sb("wgs_sb", S, F32, tag="big2")
+        w1_raw = sb("w1_raw", PASSES * 2 * H, U8, tag="zt0")
         w1_sc_raw = sb("w1_sc_raw", H, U8, tag="page2")
         planes1 = [sb("planes1_%d" % a, S + H, U8) for a in range(PASSES)]
 
@@ -79,13 +79,13 @@ def tile_list_berth_page_nowcast_kernel(
             rate_sb[:].rearrange("p (b t) -> p b t", b=PASSES), rate.rearrange("(b p t) -> p b t", b=PASSES, t=PACK)
         )
         nc.sync.dma_start(list2[:], offs2)
-        for rows, scales in [(tab_sc, tab_scales), (w1_sc_raw, w1_scales)]:
-            for a in range(PASSES):
-                nc.sync.dma_start(rows[4 * a : P : 8, :].bitcast(I32), scales[a].bitcast(I32))
         nc.sync.dma_start(
             w1_raw[:].bitcast(I32).rearrange("p (a c) -> p a c", a=PASSES),
             w1_words.bitcast(I32).rearrange("a p c -> p a c"),
         )
+        for rows, scales in [(tab_sc, tab_scales), (w1_sc_raw, w1_scales)]:
+            for a in range(PASSES):
+                nc.sync.dma_start(rows[4 * a : P : 8, :].bitcast(I32), scales[a].bitcast(I32))
         nc.sync.dma_start(wgs_sb[:], wgs)
         tab = [sb("tab%d" % a, T, I32, tag="big%d" % a) for a in range(PASSES)]
 
@@ -146,7 +146,7 @@ def tile_list_berth_page_nowcast_kernel(
         kept_sb = {}
 
         def load_kept(pair, rows):
-            kept_sb[pair] = sb("kept%d" % pair, rows * T2, F32, tag="big%d" % (pair % 2))
+            kept_sb[pair] = sb("kept%d" % pair, rows * T2, F32, tag="big%d" % (1 + pair % 2))
             nc.sync.dma_start(
                 kept_sb[pair][:].rearrange("p (e m) -> p e m", e=rows), kept_rows[pair // 2, pair % 2][:, :rows, :]
             )
@@ -206,26 +206,46 @@ def tile_list_berth_page_nowcast_kernel(
                 dst, pages[k % PAGES][:, c * P : (c + 1) * P], ident[:], start=False, stop=True, is_transpose=True
             )
 
-        def blend_pair(pair, zt):
-            for c0 in range(0, BLOCKS, 2):
-                sums = take("sum", SUM_BANKS)
+        def blend_pair(pair, zt, banks):
+            starts = list(range(0, BLOCKS, 2))
+            sums = {}
+
+            def add_tile(c0, e):
                 for cc in range(2):
-                    for e in range(2):
-                        s0 = (cc * 2 + e) * P
-                        add_block(sums[:, s0 : s0 + P], 2 * pair + e, c0 + cc)
+                    s0 = (cc * 2 + e) * P
+                    add_block(sums[c0][:, s0 : s0 + P], 2 * pair + e, c0 + cc)
+
+            def open_bank(c0):
+                sums[c0] = take("sum", banks)
+                add_tile(c0, 0)
+
+            for c0 in starts[: len(banks)]:
+                open_bank(c0)
+            for i, c0 in enumerate(starts):
+                add_tile(c0, 1)
                 nc.scalar.copy(
                     zt[:, c0 * 2 * P : (c0 + 2) * 2 * P].rearrange("m (c p e) -> m c p e", c=2, e=2),
-                    sums[:].rearrange("m (c e p) -> m c p e", c=2, e=2),
+                    sums[c0][:].rearrange("m (c e p) -> m c p e", c=2, e=2),
                 )
+                if i + len(banks) < len(starts):
+                    open_bank(starts[i + len(banks)])
 
-        def blend_low(k, zt):
-            for c0 in range(0, BLOCKS, 4):
-                sums = take("sum", SUM_BANKS)
-                for cc in range(4):
-                    add_block(sums[:, cc * P : (cc + 1) * P], k, c0 + cc)
-                nc.scalar.copy(
-                    zt[:, c0 * 2 * P : (c0 + 4) * 2 * P].rearrange("m (x e) -> m x e", e=2)[:, :, 0], sums[:]
-                )
+        def blend_low(k, zt, banks):
+            sums = [take("sum", banks) for c0 in range(0, BLOCKS, 4)]
+            for source, first in [(kept_sb[k // 2], True), (pages[k % PAGES], False)]:
+                for i, c0 in enumerate(range(0, BLOCKS, 4)):
+                    for cc in range(4):
+                        nc.tensor.matmul(
+                            sums[i][:, cc * P : (cc + 1) * P],
+                            source[:, (c0 + cc) * P : (c0 + cc + 1) * P],
+                            ident[:],
+                            start=first and cc == 0,
+                            stop=not first and cc == 3,
+                            is_transpose=True,
+                        )
+                    if not first:
+                        halves = zt[:, c0 * 2 * P : (c0 + 4) * 2 * P].rearrange("m (x e) -> m x e", e=2)
+                        nc.scalar.copy(halves[:, :, 0], sums[i][:])
 
         def words(zt, c):
             return zt[:, c * 2 * P : (c + 1) * 2 * P].bitcast(F32)
@@ -250,7 +270,7 @@ def tile_list_berth_page_nowcast_kernel(
                 w0 = u * T2 + c0 * P
                 nc.scalar.copy(dst[:, 2 * w0 : 2 * (w0 + BANK)].bitcast(F32), moved[:])
 
-        w2_raw = sb("w2_raw", PASSES * PACK * N, F32, tag="w2_raw")
+        w2_raw = sb("w2_raw", PASSES * PACK * N, F32, tag="big0")
         nc.sync.dma_start(
             w2_raw[:].rearrange("p (b x) -> p b x", b=PASSES),
             w2.rearrange("(b p j) n -> p b (j n)", b=PASSES, j=PACK),
@@ -280,7 +300,7 @@ def tile_list_berth_page_nowcast_kernel(
                 w2_raw[:, cols].rearrange("p (j m t) -> p m j t", t=PACK, j=PACK),
             )
         nc.vector.quantize_mx(out=w2_codes[:].bitcast(FP8X4), scales=w2_sc[:], in_=w2_bf[:])
-        pages.append(sb("page3", T2, F32, tag="w2_raw"))
+        pages.append(sb("page3", T2, F32, tag="big0"))
         nc.gpsimd.memset(pages[3][:], 0.0)
         scatter(3)
 
@@ -289,7 +309,7 @@ def tile_list_berth_page_nowcast_kernel(
         z1_words = sb("z1_words", PACK * T2, BF16)
 
         features(4, FEATURE_BANKS)
-        blend_pair(0, zt[0])
+        blend_pair(0, zt[0], SUM_BANKS)
         load_kept(2, 2)
         for k in range(5, TILES):
             features(k, FEATURE_BANKS)
@@ -298,15 +318,15 @@ def tile_list_berth_page_nowcast_kernel(
         for j in range(CHUNKS):
             kept_last.append(sb("kept_last%d" % j, BANK, F32, tag="strip%d" % j))
             nc.sync.dma_start(kept_last[j][:], kept_rows[1, 1][:, 1, j * BANK : (j + 1) * BANK])
-        blend_pair(1, zt[1])
+        blend_pair(1, zt[1], SUM_BANKS + FEATURE_BANKS)
         load_kept(3, 1)
         back_both(zt, z0)
         scatter(4)
         scatter(5)
-        blend_pair(2, zt[0])
+        blend_pair(2, zt[0], SUM_BANKS + FEATURE_BANKS)
         back_one(zt[0], z1_words, 0)
         scatter(6)
-        blend_low(6, zt[1])
+        blend_low(6, zt[1], SUM_BANKS + FEATURE_BANKS)
         back_one(zt[1], z1_words, 1)
         scatter(7)
 

@@ -32,7 +32,7 @@ FIRST_PIECES = [(0, 128), (128, 512), (512, 1024)]
 PARTS = [(0, 512, (0, 2)), (512, 512, (0, 2)), (1024, 512, (0, 2)), (1536, 256, ()), (1792, 256, ())]
 ROUND_RUNS = 64
 STORE_COLUMNS = 1024
-VECTOR_WEIGHS = 4
+VECTOR_WEIGHS = 3
 FEATURE_BANKS = [0, 1]
 SUM_BANKS = [2, 3, 4]
 BACK_BANKS = [5, 6, 7]
@@ -69,8 +69,8 @@ def tile_list_berth_page_nowcast_kernel(
         planes1 = [sb("planes1_%d" % a, S + H, U8) for a in range(PASSES)]
 
         nc.gpsimd.memset(tab_sc[:].bitcast(I32), 0)
+        nc.vector.memset(w1_sc_raw[:].bitcast(I32), 0)
         nc.vector.memset(one[:], 1.0)
-        nc.gpsimd.memset(w1_sc_raw[:].bitcast(I32), 0)
 
         nc.gpsimd.memset(planes1[1][:].bitcast(I32), 0)
 
@@ -108,7 +108,7 @@ def tile_list_berth_page_nowcast_kernel(
                 nc.scalar.dma_start(planes1[a][i:P:32, :].bitcast(I32), staged[8 * i + 4 * a : P : 32, :].bitcast(I32))
 
         pages = [sb("page0", T2, F32, tag="page0")]
-        nc.gpsimd.memset(pages[0][:], 0.0)
+        nc.vector.memset(pages[0][:], 0.0)
 
         make_identity(nc, ident[:])
         nc.scalar.activation(unit[:], one[:], ACT.Sqrt)
@@ -154,7 +154,7 @@ def tile_list_berth_page_nowcast_kernel(
         h = {}
 
         def features(k, banks):
-            h[k] = sb("h%d" % k, S, F32, tag="h", bufs=TILES)
+            h[k] = sb("h%d" % k, S, F32, tag="h_last") if k == TILES - 1 else sb("h%d" % k, S, F32, tag="h", bufs=TILES - 1)
             sq = sb("sq%d" % k, S, F32, tag="page%d" % (k + 1)) if k < 2 else h[k]
             spans = FIRST_PIECES if k == 0 else [(0, BANK), (BANK, S)]
             for i, (lo, hi) in enumerate(spans):
@@ -290,16 +290,13 @@ def tile_list_berth_page_nowcast_kernel(
         for k in range(3):
             scatter(k)
 
-        w2_bf = sb("w2_bf", PASSES * PACK * N, BF16, tag="zt1")
-        w2_codes = sb("w2_codes", PASSES * N, U32)
-        w2_sc = sb("w2_sc", PASSES * N, U8)
+        w2_bf = sb("w2_bf", PASSES * PACK * N, BF16)
         for b in range(PASSES):
             cols = slice(b * PACK * N, (b + 1) * PACK * N)
             nc.scalar.copy(
                 w2_bf[:, cols].rearrange("p (t m j) -> p m j t", t=PACK, j=PACK),
                 w2_raw[:, cols].rearrange("p (j m t) -> p m j t", t=PACK, j=PACK),
             )
-        nc.vector.quantize_mx(out=w2_codes[:].bitcast(FP8X4), scales=w2_sc[:], in_=w2_bf[:])
         pages.append(sb("page3", T2, F32, tag="big0"))
         nc.gpsimd.memset(pages[3][:], 0.0)
         scatter(3)
@@ -350,7 +347,7 @@ def tile_list_berth_page_nowcast_kernel(
                 kept_last[j][:],
                 ALU.add,
             )
-            z1[j] = sb("z1_%d" % j, PACK * BANK, BF16, tag="h", bufs=TILES)
+            z1[j] = sb("z1_%d" % j, PACK * BANK, BF16, tag="h", bufs=TILES - 1)
             nc.scalar.copy(
                 z1[j][:].bitcast(F32).rearrange("p (m u) -> p m u", u=2),
                 z1_words[:].bitcast(F32).rearrange("p (u m) -> p m u", u=2)[:, span(j), :],
@@ -402,7 +399,7 @@ def tile_list_berth_page_nowcast_kernel(
 
         def round_y(i):
             width = PARTS[i][1]
-            y_bf[i] = sb("y_bf%d" % i, PACK * width, BF16, tag="h", bufs=TILES)
+            y_bf[i] = sb("y_bf%d" % i, PACK * width, BF16, tag="h", bufs=TILES - 1)
             rounded = y_bf[i][:].rearrange("p (c i t) -> p c t i", t=PACK, i=4)
             by_column = y[i][:].rearrange("p (t c i) -> p c t i", t=PACK, i=4)
             if i == len(PARTS) - 1:
@@ -418,6 +415,9 @@ def tile_list_berth_page_nowcast_kernel(
             nc.sync.dma_start(y_words[:, cols], y_codes[:, cols].bitcast(I32))
 
         finish_z(0)
+        w2_codes = sb("w2_codes", PASSES * N, U32, tag="h_last")
+        w2_sc = sb("w2_sc", PASSES * N, U8)
+        nc.vector.quantize_mx(out=w2_codes[:].bitcast(FP8X4), scales=w2_sc[:], in_=w2_bf[:])
         finish_z(1)
         quantise_z(0)
         finish_z(2)

@@ -83,10 +83,10 @@ def tile_list_berth_page_nowcast_kernel(
             w1_raw[:].bitcast(I32).rearrange("p (a c) -> p a c", a=PASSES),
             w1_words.bitcast(I32).rearrange("a p c -> p a c"),
         )
+        nc.sync.dma_start(wgs_sb[:], wgs)
         for rows, scales in [(tab_sc, tab_scales), (w1_sc_raw, w1_scales)]:
             for a in range(PASSES):
                 nc.sync.dma_start(rows[4 * a : P : 8, :].bitcast(I32), scales[a].bitcast(I32))
-        nc.sync.dma_start(wgs_sb[:], wgs)
         tab = [sb("tab%d" % a, T, I32, tag="big%d" % a) for a in range(PASSES)]
 
         def load_table(a):

@@ -33,6 +33,9 @@ PARTS = [(0, 512, (0, 2)), (512, 512, (0, 2)), (1024, 512, (0, 2)), (1536, 256, 
 ROUND_RUNS = 64
 STORE_COLUMNS = 1024
 VECTOR_WEIGHS = 3
+TABLE_AHEAD = 1024
+LAST_PAIR_BANKS = [0, 1, 2, 3]
+LOW_BANKS = [4, 5, 6, 7]
 FEATURE_BANKS = [0, 1]
 SUM_BANKS = [2, 3, 4]
 BACK_BANKS = [5, 6, 7]
@@ -74,26 +77,27 @@ def tile_list_berth_page_nowcast_kernel(
 
         nc.gpsimd.memset(planes1[1][:].bitcast(I32), 0)
 
-        nc.sync.dma_start(list1[:], offs)
         nc.scalar.dma_start(
             rate_sb[:].rearrange("p (b t) -> p b t", b=PASSES), rate.rearrange("(b p t) -> p b t", b=PASSES, t=PACK)
         )
-        nc.sync.dma_start(list2[:], offs2)
         nc.sync.dma_start(
             w1_raw[:].bitcast(I32).rearrange("p (a c) -> p a c", a=PASSES),
             w1_words.bitcast(I32).rearrange("a p c -> p a c"),
         )
+        nc.sync.dma_start(list1[:], offs)
         nc.sync.dma_start(wgs_sb[:], wgs)
+        tab = [sb("tab%d" % a, T, I32, tag="big%d" % a) for a in range(PASSES)]
+
+        def load_table(a, lo, hi):
+            nc.sync.dma_start(tab[a][:, lo:hi], tab_words[a].rearrange("p c i -> p (c i)").bitcast(I32)[:, lo:hi])
+
+        load_table(0, 0, TABLE_AHEAD)
+        nc.sync.dma_start(list2[:], offs2)
         for rows, scales in [(tab_sc, tab_scales), (w1_sc_raw, w1_scales)]:
             for a in range(PASSES):
                 nc.sync.dma_start(rows[4 * a : P : 8, :].bitcast(I32), scales[a].bitcast(I32))
-        tab = [sb("tab%d" % a, T, I32, tag="big%d" % a) for a in range(PASSES)]
-
-        def load_table(a):
-            nc.sync.dma_start(tab[a][:], tab_words[a].rearrange("p c i -> p (c i)").bitcast(I32))
-
-        load_table(0)
-        load_table(1)
+        load_table(0, TABLE_AHEAD, T)
+        load_table(1, 0, T)
 
         staged = planes1[0]
         v_rows = sb("v_rows", S, U8)
@@ -199,30 +203,37 @@ def tile_list_berth_page_nowcast_kernel(
             turn[kind] = i + 1
             return bank(banks[i % len(banks)], "%s%d" % (kind, i))
 
-        def add_block(dst, k, c):
-            k0 = (k % 2) * T2 + c * P
-            nc.tensor.matmul(dst, kept_sb[k // 2][:, k0 : k0 + P], ident[:], start=True, stop=False, is_transpose=True)
-            nc.tensor.matmul(
-                dst, pages[k % PAGES][:, c * P : (c + 1) * P], ident[:], start=False, stop=True, is_transpose=True
-            )
-
-        def blend_pair(pair, zt, banks):
+        def blend_pair(pair, zt, banks, kept_ahead, meanwhile=None):
             starts = list(range(0, BLOCKS, 2))
             sums = {}
 
-            def add_tile(c0, e):
+            def add_on(c0, source, e, first=False, last=False):
                 for cc in range(2):
                     s0 = (cc * 2 + e) * P
-                    add_block(sums[c0][:, s0 : s0 + P], 2 * pair + e, c0 + cc)
+                    nc.tensor.matmul(
+                        sums[c0][:, s0 : s0 + P],
+                        source[:, (c0 + cc) * P : (c0 + cc + 1) * P],
+                        ident[:],
+                        start=first and cc == 0,
+                        stop=last and cc == 1,
+                        is_transpose=True,
+                    )
 
             def open_bank(c0):
-                sums[c0] = take("sum", banks)
-                add_tile(c0, 0)
+                sums[c0] = bank(banks[starts.index(c0) % len(banks)], "sum%d_%d" % (pair, c0))
+                add_on(c0, kept_sb[pair][:, :T2], 0, first=True)
+                add_on(c0, pages[2 * pair % PAGES], 0)
+                if kept_ahead:
+                    add_on(c0, kept_sb[pair][:, T2:], 1)
 
             for c0 in starts[: len(banks)]:
                 open_bank(c0)
+            if meanwhile is not None:
+                meanwhile()
             for i, c0 in enumerate(starts):
-                add_tile(c0, 1)
+                if not kept_ahead:
+                    add_on(c0, kept_sb[pair][:, T2:], 1)
+                add_on(c0, pages[(2 * pair + 1) % PAGES], 1, last=True)
                 nc.scalar.copy(
                     zt[:, c0 * 2 * P : (c0 + 2) * 2 * P].rearrange("m (c p e) -> m c p e", c=2, e=2),
                     sums[c0][:].rearrange("m (c e p) -> m c p e", c=2, e=2),
@@ -230,29 +241,31 @@ def tile_list_berth_page_nowcast_kernel(
                 if i + len(banks) < len(starts):
                     open_bank(starts[i + len(banks)])
 
-        def blend_low(k, zt, banks):
-            sums = [take("sum", banks) for c0 in range(0, BLOCKS, 4)]
-            for source, first in [(kept_sb[k // 2], True), (pages[k % PAGES], False)]:
-                for i, c0 in enumerate(range(0, BLOCKS, 4)):
-                    for cc in range(4):
-                        nc.tensor.matmul(
-                            sums[i][:, cc * P : (cc + 1) * P],
-                            source[:, (c0 + cc) * P : (c0 + cc + 1) * P],
-                            ident[:],
-                            start=first and cc == 0,
-                            stop=not first and cc == 3,
-                            is_transpose=True,
-                        )
-                    if not first:
-                        halves = zt[:, c0 * 2 * P : (c0 + 4) * 2 * P].rearrange("m (x e) -> m x e", e=2)
-                        nc.scalar.copy(halves[:, :, 0], sums[i][:])
+        low = []
+
+        def add_low(source, first):
+            for i, c0 in enumerate(range(0, BLOCKS, 4)):
+                if first:
+                    low.append(bank(LOW_BANKS[i], "low%d" % i))
+                for cc in range(4):
+                    nc.tensor.matmul(
+                        low[i][:, cc * P : (cc + 1) * P],
+                        source[:, (c0 + cc) * P : (c0 + cc + 1) * P],
+                        ident[:],
+                        start=first and cc == 0,
+                        stop=not first and cc == 3,
+                        is_transpose=True,
+                    )
+                if not first:
+                    halves = zt[1][:, c0 * 2 * P : (c0 + 4) * 2 * P].rearrange("m (x e) -> m x e", e=2)
+                    nc.scalar.copy(halves[:, :, 0], low[i][:])
 
         def words(zt, c):
             return zt[:, c * 2 * P : (c + 1) * 2 * P].bitcast(F32)
 
         def back_both(zts, dst):
             for c0 in range(0, BLOCKS, 2):
-                moved = take("back", BACK_BANKS)
+                moved = take("back", FEATURE_BANKS + BACK_BANKS)
                 for u in range(2):
                     for cc in range(2):
                         s0 = (u * 2 + cc) * P
@@ -264,7 +277,7 @@ def tile_list_berth_page_nowcast_kernel(
 
         def back_one(zt, dst, u):
             for c0 in range(0, BLOCKS, 4):
-                moved = take("back", BACK_BANKS)
+                moved = bank(LAST_PAIR_BANKS[c0 // 4], "back_one%d_%d" % (u, c0))
                 for cc in range(4):
                     nc.tensor.transpose(moved[:, cc * P : (cc + 1) * P], words(zt, c0 + cc), ident[:])
                 w0 = u * T2 + c0 * P
@@ -306,7 +319,7 @@ def tile_list_berth_page_nowcast_kernel(
         z1_words = sb("z1_words", PACK * T2, BF16)
 
         features(4, FEATURE_BANKS)
-        blend_pair(0, zt[0], SUM_BANKS)
+        blend_pair(0, zt[0], SUM_BANKS + BACK_BANKS, True)
         load_kept(2, 2)
         for k in range(5, TILES):
             features(k, FEATURE_BANKS)
@@ -315,15 +328,15 @@ def tile_list_berth_page_nowcast_kernel(
         for j in range(CHUNKS):
             kept_last.append(sb("kept_last%d" % j, BANK, F32, tag="strip%d" % j))
             nc.sync.dma_start(kept_last[j][:], kept_rows[1, 1][:, 1, j * BANK : (j + 1) * BANK])
-        blend_pair(1, zt[1], SUM_BANKS + FEATURE_BANKS)
+        blend_pair(1, zt[1], SUM_BANKS + BACK_BANKS, True)
         load_kept(3, 1)
         back_both(zt, z0)
         scatter(4)
         scatter(5)
-        blend_pair(2, zt[0], SUM_BANKS + FEATURE_BANKS)
+        blend_pair(2, zt[0], LAST_PAIR_BANKS, False, lambda: add_low(kept_sb[3], True))
         back_one(zt[0], z1_words, 0)
         scatter(6)
-        blend_low(6, zt[1], SUM_BANKS + FEATURE_BANKS)
+        add_low(pages[2], False)
         back_one(zt[1], z1_words, 1)
         scatter(7)
 

@@ -29,16 +29,16 @@ GROUP = 16
 QUADS = 4
 ALIGN = 64
 FIRST_PIECES = [(0, 128), (128, 512), (512, 1024)]
-PARTS = [(0, 512, (0, 2)), (512, 512, (0, 2)), (1024, 512, (0, 2)), (1536, 256, ()), (1792, 256, ())]
+PARTS = [(0, 512, (1, 3)), (512, 512, (1, 3)), (1024, 512, (1, 3)), (1536, 256, ()), (1792, 256, ())]
 ROUND_RUNS = 64
 STORE_COLUMNS = 1024
 VECTOR_WEIGHS = 3
 TABLE_AHEAD = 1024
-LAST_PAIR_BANKS = [0, 1, 2, 3]
-LOW_BANKS = [4, 5, 6, 7]
 FEATURE_BANKS = [0, 1]
-SUM_BANKS = [2, 3, 4]
-BACK_BANKS = [5, 6, 7]
+PAIR_BANKS = [[2, 3, 4, 5, 6, 7], [2, 3, 4, 5, 6, 7, 0, 1], [5, 6, 7, 0]]
+BACK_BANKS = [2, 3, 4]
+LOW_BANKS = [1, 2, 3, 4]
+LAST_PAIR_BANKS = PAIR_BANKS[2]
 
 
 def tile_list_berth_page_nowcast_kernel(
@@ -117,7 +117,7 @@ def tile_list_berth_page_nowcast_kernel(
         make_identity(nc, ident[:])
         nc.scalar.activation(unit[:], one[:], ACT.Sqrt)
 
-        w1_codes = sb("w1_codes", PASSES * 2 * H, U8)
+        w1_codes = sb("w1_codes", PASSES * 2 * H, U8, tag="weights")
         nc.vector.tensor_copy(
             w1_codes[:].bitcast(U16).rearrange("p (g t m) -> p g t m", t=PACK, m=P),
             w1_raw[:].bitcast(U16).rearrange("p (g m t) -> p g t m", t=PACK, m=P),
@@ -150,7 +150,7 @@ def tile_list_berth_page_nowcast_kernel(
         kept_sb = {}
 
         def load_kept(pair, rows):
-            kept_sb[pair] = sb("kept%d" % pair, rows * T2, F32, tag="big%d" % (1 + pair % 2))
+            kept_sb[pair] = sb("kept%d" % pair, rows * T2, F32, tag="big%d" % (2 * (pair % 2)))
             nc.sync.dma_start(
                 kept_sb[pair][:].rearrange("p (e m) -> p e m", e=rows), kept_rows[pair // 2, pair % 2][:, :rows, :]
             )
@@ -196,50 +196,46 @@ def tile_list_berth_page_nowcast_kernel(
                     ALU.mult,
                 )
 
-        turn = {"sum": 0, "back": 0}
+        sums = {}
 
-        def take(kind, banks):
-            i = turn[kind]
-            turn[kind] = i + 1
-            return bank(banks[i % len(banks)], "%s%d" % (kind, i))
-
-        def blend_pair(pair, zt, banks, kept_ahead, meanwhile=None):
-            starts = list(range(0, BLOCKS, 2))
-            sums = {}
-
-            def add_on(c0, source, e, first=False, last=False):
-                for cc in range(2):
-                    s0 = (cc * 2 + e) * P
-                    nc.tensor.matmul(
-                        sums[c0][:, s0 : s0 + P],
-                        source[:, (c0 + cc) * P : (c0 + cc + 1) * P],
-                        ident[:],
-                        start=first and cc == 0,
-                        stop=last and cc == 1,
-                        is_transpose=True,
-                    )
-
-            def open_bank(c0):
-                sums[c0] = bank(banks[starts.index(c0) % len(banks)], "sum%d_%d" % (pair, c0))
-                add_on(c0, kept_sb[pair][:, :T2], 0, first=True)
-                add_on(c0, pages[2 * pair % PAGES], 0)
-                if kept_ahead:
-                    add_on(c0, kept_sb[pair][:, T2:], 1)
-
-            for c0 in starts[: len(banks)]:
-                open_bank(c0)
-            if meanwhile is not None:
-                meanwhile()
-            for i, c0 in enumerate(starts):
-                if not kept_ahead:
-                    add_on(c0, kept_sb[pair][:, T2:], 1)
-                add_on(c0, pages[(2 * pair + 1) % PAGES], 1, last=True)
-                nc.scalar.copy(
-                    zt[:, c0 * 2 * P : (c0 + 2) * 2 * P].rearrange("m (c p e) -> m c p e", c=2, e=2),
-                    sums[c0][:].rearrange("m (c e p) -> m c p e", c=2, e=2),
+        def add_on(pair, g, source, e, first=False, last=False):
+            for cc in range(2):
+                s0, c0 = (cc * 2 + e) * P, (2 * g + cc) * P
+                nc.tensor.matmul(
+                    sums[pair, g][:, s0 : s0 + P],
+                    source[:, c0 : c0 + P],
+                    ident[:],
+                    start=first and cc == 0,
+                    stop=last and cc == 1,
+                    is_transpose=True,
                 )
-                if i + len(banks) < len(starts):
-                    open_bank(starts[i + len(banks)])
+
+        def add_kept(pair, groups):
+            for g in groups:
+                banks = PAIR_BANKS[pair]
+                sums[pair, g] = bank(banks[g % len(banks)], "sum%d_%d" % (pair, g))
+                add_on(pair, g, kept_sb[pair][:, :T2], 0, first=True)
+                if pair < 2:
+                    add_on(pair, g, kept_sb[pair][:, T2:], 1)
+
+        def add_even(pair, groups):
+            for g in groups:
+                add_on(pair, g, pages[2 * pair % PAGES], 0)
+
+        def close_pair(pair, zt):
+            ahead = len(PAIR_BANKS[pair])
+            for g in range(BLOCKS // 2):
+                if pair == 2:
+                    add_on(pair, g, kept_sb[pair][:, T2:], 1)
+                add_on(pair, g, pages[(2 * pair + 1) % PAGES], 1, last=True)
+                nc.scalar.copy(
+                    zt[:, g * 4 * P : (g + 1) * 4 * P].rearrange("m (c p e) -> m c p e", c=2, e=2),
+                    sums[pair, g][:].rearrange("m (c e p) -> m c p e", c=2, e=2),
+                )
+                again = g - 2 + ahead
+                if ahead <= again < BLOCKS // 2:
+                    add_kept(pair, [again])
+                    add_even(pair, [again])
 
         low = []
 
@@ -263,9 +259,9 @@ def tile_list_berth_page_nowcast_kernel(
         def words(zt, c):
             return zt[:, c * 2 * P : (c + 1) * 2 * P].bitcast(F32)
 
-        def back_both(zts, dst):
-            for c0 in range(0, BLOCKS, 2):
-                moved = take("back", FEATURE_BANKS + BACK_BANKS)
+        def back_both(zts, dst, groups):
+            for c0 in [2 * g for g in groups]:
+                moved = bank(BACK_BANKS[c0 // 2 % len(BACK_BANKS)], "back%d" % c0)
                 for u in range(2):
                     for cc in range(2):
                         s0 = (u * 2 + cc) * P
@@ -283,57 +279,67 @@ def tile_list_berth_page_nowcast_kernel(
                 w0 = u * T2 + c0 * P
                 nc.scalar.copy(dst[:, 2 * w0 : 2 * (w0 + BANK)].bitcast(F32), moved[:])
 
-        w2_raw = sb("w2_raw", PASSES * PACK * N, F32, tag="big0")
+        load_kept(0, 2)
+        load_kept(1, 2)
+        w2_raw = sb("w2_raw", PASSES * PACK * N, F32, tag="big1")
         nc.sync.dma_start(
             w2_raw[:].rearrange("p (b x) -> p b x", b=PASSES),
             w2.rearrange("(b p j) n -> p b (j n)", b=PASSES, j=PACK),
         )
-        load_kept(0, 2)
-        load_kept(1, 2)
         nc.sync.dma_start(floor_sb[:], floor.rearrange("(p t) -> p t", t=PACK))
 
         for k in range(VECTOR_WEIGHS):
             weigh(k)
-        features(0, SUM_BANKS[:1] + FEATURE_BANKS)
+        features(0, [2] + FEATURE_BANKS)
         features(1, FEATURE_BANKS)
         for k in range(VECTOR_WEIGHS, TILES):
             weigh(k)
-        features(2, FEATURE_BANKS)
-        features(3, FEATURE_BANKS)
-        for k in range(3):
-            scatter(k)
+        pages.append(sb("page3", T2, F32, tag="page3"))
+        nc.gpsimd.memset(pages[3][:], 0.0)
+        zt = [sb("zt%d" % u, BLOCKS * 2 * P, BF16, tag="zt%d" % u) for u in range(2)]
+        z0 = sb("z0", PACK * T2, BF16)
+        z1_words = sb("z1_words", PACK * T2, BF16)
 
-        w2_bf = sb("w2_bf", PASSES * PACK * N, BF16)
+        features(2, FEATURE_BANKS)
+        scatter(0)
+        scatter(1)
+        scatter(2)
+        features(3, FEATURE_BANKS)
+        add_kept(0, range(3))
+        scatter(3)
+        features(4, FEATURE_BANKS)
+        add_kept(0, range(3, 6))
+        features(5, FEATURE_BANKS)
+        add_even(0, range(6))
+        features(6, FEATURE_BANKS)
+        close_pair(0, zt[0])
+        load_kept(2, 2)
+        features(7, FEATURE_BANKS)
+
+        w2_bf = sb("w2_bf", PASSES * PACK * N, BF16, tag="weights")
         for b in range(PASSES):
             cols = slice(b * PACK * N, (b + 1) * PACK * N)
             nc.scalar.copy(
                 w2_bf[:, cols].rearrange("p (t m j) -> p m j t", t=PACK, j=PACK),
                 w2_raw[:, cols].rearrange("p (j m t) -> p m j t", t=PACK, j=PACK),
             )
-        pages.append(sb("page3", T2, F32, tag="big0"))
-        nc.gpsimd.memset(pages[3][:], 0.0)
-        scatter(3)
-
-        zt = [sb("zt%d" % u, BLOCKS * 2 * P, BF16, tag="zt%d" % u) for u in range(2)]
-        z0 = sb("z0", PACK * T2, BF16)
-        z1_words = sb("z1_words", PACK * T2, BF16)
-
-        features(4, FEATURE_BANKS)
-        blend_pair(0, zt[0], SUM_BANKS + BACK_BANKS, True)
-        load_kept(2, 2)
-        for k in range(5, TILES):
-            features(k, FEATURE_BANKS)
         last = TILES - 1
         kept_last = []
         for j in range(CHUNKS):
             kept_last.append(sb("kept_last%d" % j, BANK, F32, tag="strip%d" % j))
             nc.sync.dma_start(kept_last[j][:], kept_rows[1, 1][:, 1, j * BANK : (j + 1) * BANK])
-        blend_pair(1, zt[1], SUM_BANKS + BACK_BANKS, True)
+        add_kept(1, range(8))
         load_kept(3, 1)
-        back_both(zt, z0)
+        add_even(1, range(8))
+        close_pair(1, zt[1])
         scatter(4)
         scatter(5)
-        blend_pair(2, zt[0], LAST_PAIR_BANKS, False, lambda: add_low(kept_sb[3], True))
+        back_both(zt, z0, range(3))
+        add_kept(2, range(4))
+        back_both(zt, z0, range(3, 8))
+        add_even(2, range(4))
+        add_low(kept_sb[3], True)
+        close_pair(2, zt[0])
         back_one(zt[0], z1_words, 0)
         scatter(6)
         add_low(pages[2], False)

@@ -28,7 +28,8 @@ CHUNKS = T2 // BANK
 GROUP = 16
 QUADS = 4
 ALIGN = 64
-FIRST_PIECES = [(0, 128), (128, 512), (512, 1024)]
+FIRST_PIECES = [(0, 128), (128, 256, 512), (512, 1024)]
+LAST_GATHERS = [(0, 256), (256, 512), (512, 1024)]
 PARTS = [(0, 512, (1, 3)), (512, 512, (1, 3)), (1024, 512, (1, 3)), (1536, 256, ()), (1792, 256, ())]
 ROUND_RUNS = 64
 STORE_COLUMNS = 1024
@@ -65,9 +66,9 @@ def tile_list_berth_page_nowcast_kernel(
         one = sb("one", 1, F32)
         unit = sb("unit", 1, F32)
         ident = sb("ident", P, F32)
-        tab_sc = sb("tab_sc", T, U8, tag="page1")
+        tab_sc = sb("tab_sc", T, U8, tag="page3")
         wgs_sb = sb("wgs_sb", S, F32, tag="big2")
-        w1_raw = sb("w1_raw", PASSES * 2 * H, U8, tag="zt0")
+        w1_raw = sb("w1_raw", PASSES * 2 * H, U8, tag="page1")
         w1_sc_raw = sb("w1_sc_raw", H, U8, tag="page2")
         planes1 = [sb("planes1_%d" % a, S + H, U8) for a in range(PASSES)]
 
@@ -123,19 +124,21 @@ def tile_list_berth_page_nowcast_kernel(
             w1_raw[:].bitcast(U16).rearrange("p (g m t) -> p g t m", t=PACK, m=P),
         )
 
+        pages.append(sb("page1", T2, F32, tag="page1"))
+        nc.gpsimd.memset(pages[1][:], 0.0)
+
         v_codes = []
 
-        def gather_words(a):
-            halves = []
-            for i in range(S // BANK):
-                half = sb("v_codes%d_%d" % (a, i), BANK, U32, tag="strip%d" % (2 * a + i))
-                offsets = list1[:, i * BANK // GROUP : (i + 1) * BANK // GROUP]
-                nc.vector.tensor_copy(half[:], tab[a][:].bitcast(U32).indirect(offsets))
-                halves.append(half)
+        def gather_words(a, spans):
+            halves = [sb("v_codes%d_%d" % (a, i), BANK, U32, tag="strip%d" % (2 * a + i)) for i in range(S // BANK)]
+            for lo, hi in spans:
+                offsets = list1[:, lo // GROUP : hi // GROUP]
+                c0 = lo % BANK
+                nc.vector.tensor_copy(halves[lo // BANK][:, c0 : c0 + hi - lo], tab[a][:].bitcast(U32).indirect(offsets))
             v_codes.append(halves)
 
-        gather_words(0)
-        gather_words(1)
+        gather_words(0, [(0, BANK), (BANK, S)])
+        gather_words(1, LAST_GATHERS)
 
         rw = [sb("rw%d" % i, 2 * S, F32, tag="rw", bufs=4) for i in range(TILES // 2)]
 
@@ -157,44 +160,57 @@ def tile_list_berth_page_nowcast_kernel(
 
         h = {}
 
-        def features(k, banks):
+        def product(k, acc, lo, hi, at):
+            for a in range(PASSES):
+                c0 = a * H + k * P
+                nc.tensor.matmul_mx(
+                    out=acc[:, at : at + hi - lo],
+                    lhsT=w1_codes[:, 2 * c0 : 2 * (c0 + P)].bitcast(FP4X4),
+                    lhsT_scale=planes1[a][:, S + k * P : S + (k + 1) * P],
+                    rhs=v_codes[a][lo // BANK][:, lo % BANK : lo % BANK + hi - lo].bitcast(FP8X4),
+                    rhs_scale=planes1[a][:, lo:hi],
+                    start=(a == 0),
+                    stop=(a == PASSES - 1),
+                )
+
+        def h_tile(k):
             h[k] = sb("h%d" % k, S, F32, tag="h_last") if k == TILES - 1 else sb("h%d" % k, S, F32, tag="h", bufs=TILES - 1)
-            sq = sb("sq%d" % k, S, F32, tag="page%d" % (k + 1)) if k < 2 else h[k]
-            spans = FIRST_PIECES if k == 0 else [(0, BANK), (BANK, S)]
+
+        def features(k, banks):
+            h_tile(k)
+            spans = [(0, BANK), (BANK, S)]
             for i, (lo, hi) in enumerate(spans):
                 acc = bank(banks[i], "a%d_%d" % (k, i))
-                width = BANK if hi - lo == BANK else P
-                for n0 in range(lo, hi, width):
-                    for a in range(PASSES):
-                        c0 = a * H + k * P
-                        nc.tensor.matmul_mx(
-                            out=acc[:, n0 - lo : n0 - lo + width],
-                            lhsT=w1_codes[:, 2 * c0 : 2 * (c0 + P)].bitcast(FP4X4),
-                            lhsT_scale=planes1[a][:, S + k * P : S + (k + 1) * P],
-                            rhs=v_codes[a][n0 // BANK][:, n0 % BANK : n0 % BANK + width].bitcast(FP8X4),
-                            rhs_scale=planes1[a][:, n0 : n0 + width],
-                            start=(a == 0),
-                            stop=(a == PASSES - 1),
-                        )
-                nc.scalar.activation(sq[:, lo:hi], acc[:, : hi - lo], ACT.Square)
-                if k == 0:
-                    nc.scalar.activation(h[k][:, lo:hi], sq[:, lo:hi], ACT.Sqrt, bias=unit[:])
-            if k > 0:
-                for lo, hi in spans:
-                    nc.scalar.activation(h[k][:, lo:hi], sq[:, lo:hi], ACT.Sqrt, bias=unit[:])
-            if k < 2:
-                pages.append(sb("page%d" % (k + 1), T2, F32, tag="page%d" % (k + 1)))
-                nc.gpsimd.memset(pages[k + 1][:], 0.0)
+                product(k, acc, lo, hi, 0)
+                nc.scalar.activation(h[k][:, lo:hi], acc[:], ACT.Square)
+            for lo, hi in spans:
+                nc.scalar.activation(h[k][:, lo:hi], h[k][:, lo:hi], ACT.Sqrt, bias=unit[:])
 
-        def scatter(k):
+        def scatter(k, lo=0, hi=S):
             c0 = (k % 2) * S
-            for lo, hi in FIRST_PIECES if k == 0 else [(0, S)]:
-                nc.vector.tensor_tensor(
-                    pages[k % PAGES][:].indirect(list2[:, lo // GROUP : hi // GROUP]),
-                    h[k][:, lo:hi],
-                    rw[k // 2][:, c0 + lo : c0 + hi],
-                    ALU.mult,
-                )
+            nc.vector.tensor_tensor(
+                pages[k % PAGES][:].indirect(list2[:, lo // GROUP : hi // GROUP]),
+                h[k][:, lo:hi],
+                rw[k // 2][:, c0 + lo : c0 + hi],
+                ALU.mult,
+            )
+
+        def first_pair():
+            for k in range(2):
+                h_tile(k)
+            for i, runs in enumerate(FIRST_PIECES):
+                lo, hi = runs[0], runs[-1]
+                for k in range(2):
+                    acc = bank((2 * i + k) % 4, "a%d_%d" % (k, i))
+                    for n0, n1 in zip(runs, runs[1:]):
+                        product(k, acc, n0, n1, n0 - lo)
+                    sq = sb("sq%d_%d" % (k, i), hi - lo, F32, tag="page%d" % (k + 2))
+                    nc.scalar.activation(sq[:], acc[:, : hi - lo], ACT.Square)
+                    nc.scalar.activation(h[k][:, lo:hi], sq[:], ACT.Sqrt, bias=unit[:])
+                    scatter(k, lo, hi)
+            for i in (2, 3):
+                pages.append(sb("page%d" % i, T2, F32, tag="page%d" % i))
+                nc.gpsimd.memset(pages[i][:], 0.0)
 
         sums = {}
 
@@ -290,19 +306,14 @@ def tile_list_berth_page_nowcast_kernel(
 
         for k in range(VECTOR_WEIGHS):
             weigh(k)
-        features(0, [2] + FEATURE_BANKS)
-        features(1, FEATURE_BANKS)
         for k in range(VECTOR_WEIGHS, TILES):
             weigh(k)
-        pages.append(sb("page3", T2, F32, tag="page3"))
-        nc.gpsimd.memset(pages[3][:], 0.0)
+        first_pair()
         zt = [sb("zt%d" % u, BLOCKS * 2 * P, BF16, tag="zt%d" % u) for u in range(2)]
         z0 = sb("z0", PACK * T2, BF16)
         z1_words = sb("z1_words", PACK * T2, BF16)
 
         features(2, FEATURE_BANKS)
-        scatter(0)
-        scatter(1)
         scatter(2)
         features(3, FEATURE_BANKS)
         add_kept(0, range(3))

@@ -33,7 +33,7 @@ LAST_GATHERS = [(0, 256), (256, 512), (512, 1024)]
 PARTS = [(0, 512, (1, 3)), (512, 512, (1, 3)), (1024, 512, (1, 3)), (1536, 256, ()), (1792, 256, ())]
 ROUND_RUNS = 64
 STORE_COLUMNS = 1024
-VECTOR_WEIGHS = 3
+VECTOR_WEIGHS = 5
 TABLE_AHEAD = 1024
 FEATURE_BANKS = [0, 1]
 PAIR_BANKS = [[2, 3, 4, 5, 6, 7], [2, 3, 4, 5, 6, 7, 0, 1], [5, 6, 7, 0]]
@@ -68,7 +68,7 @@ def tile_list_berth_page_nowcast_kernel(
         ident = sb("ident", P, F32)
         tab_sc = sb("tab_sc", T, U8, tag="page3")
         wgs_sb = sb("wgs_sb", S, F32, tag="big2")
-        w1_raw = sb("w1_raw", PASSES * 2 * H, U8, tag="page1")
+        w1_raw = sb("w1_raw", PASSES * 2 * H, U8, tag="zt0")
         w1_sc_raw = sb("w1_sc_raw", H, U8, tag="page2")
         planes1 = [sb("planes1_%d" % a, S + H, U8) for a in range(PASSES)]
 
@@ -101,7 +101,7 @@ def tile_list_berth_page_nowcast_kernel(
         load_table(1, 0, T)
 
         staged = planes1[0]
-        v_rows = sb("v_rows", S, U8)
+        v_rows = sb("v_rows", S, U8, tag="page1")
         nc.vector.tensor_copy(v_rows[:], tab_sc[:].indirect(list1[:]))
         nc.vector.tensor_copy(
             staged[:, S:].rearrange("p (b t m) -> p b t m", t=PACK, m=P),
@@ -119,7 +119,7 @@ def tile_list_berth_page_nowcast_kernel(
         nc.scalar.activation(unit[:], one[:], ACT.Sqrt)
 
         w1_codes = sb("w1_codes", PASSES * 2 * H, U8, tag="weights")
-        nc.vector.tensor_copy(
+        nc.scalar.copy(
             w1_codes[:].bitcast(U16).rearrange("p (g t m) -> p g t m", t=PACK, m=P),
             w1_raw[:].bitcast(U16).rearrange("p (g m t) -> p g t m", t=PACK, m=P),
         )
@@ -361,7 +361,7 @@ def tile_list_berth_page_nowcast_kernel(
         z1_codes = sb("z1_codes", T2, U32, tag="page0")
         z1_sc = sb("z1_sc", T2, U8)
         y_codes = sb("y_codes", T2, U32)
-        y_sc = sb("y_sc", T2, U8)
+        y_sc = sb("y_sc", BANK, U8)
         y_rows = out_0.rearrange("(p t) m -> p t m", t=PACK)
         y_words = out_1[0].rearrange("p m t -> p (m t)").bitcast(I32)
         z0_codes, z1, y, y_bf = {}, {}, {}, {}
@@ -441,7 +441,8 @@ def tile_list_berth_page_nowcast_kernel(
         def planes(i):
             lo, width, by_scalar = PARTS[i]
             cols = slice(lo, lo + width)
-            nc.vector.quantize_mx(out=y_codes[:, cols].bitcast(FP8X4), scales=y_sc[:, cols], in_=y_bf[i][:])
+            plane = y_sc[4 * (lo // BANK) :, lo % BANK : lo % BANK + width]
+            nc.vector.quantize_mx(out=y_codes[:, cols].bitcast(FP8X4), scales=plane, in_=y_bf[i][:])
             nc.sync.dma_start(y_words[:, cols], y_codes[:, cols].bitcast(I32))
 
         finish_z(0)
@@ -467,4 +468,5 @@ def tile_list_berth_page_nowcast_kernel(
         planes(len(PARTS) - 1)
         for q in range(QUADS):
             queue = nc.sync if q % 2 == 0 else nc.scalar
-            queue.dma_start(out_2[0, 4 * q : 4 * q + 4, :].bitcast(I32), y_sc[32 * q : 32 * q + 4, :].bitcast(I32))
+            rows = out_2[0, 4 * q : 4 * q + 4, :].bitcast(I32).rearrange("r (j c) -> j r c", j=CHUNKS)
+            queue.dma_start(rows, y_sc[32 * q : 32 * q + 16, :].bitcast(I32))

@@ -384,7 +384,7 @@ def tile_list_berth_page_nowcast_kernel(
             )
 
         def quantise_z(j):
-            z0_codes[j] = sb("z0_codes%d" % j, BANK, U32, tag="strip%d" % j)
+            z0_codes[j] = sb("z0_codes%d" % j, BANK, U32, tag="strip%d" % (j + 1) if j + 1 < CHUNKS else "page3")
             nc.vector.quantize_mx(
                 out=z0_codes[j][:].bitcast(FP8X4),
                 scales=z0_sc[:, span(j)],
@@ -406,7 +406,7 @@ def tile_list_berth_page_nowcast_kernel(
                     c0 = b * N + t * P
                     nc.tensor.matmul_mx(
                         out=acc[t][:, :width],
-                        lhsT=w2_codes[:, c0 : c0 + P].bitcast(FP8X4),
+                        lhsT=w2_codes[b][:, t * P : (t + 1) * P].bitcast(FP8X4),
                         lhsT_scale=w2_sc[:, c0 : c0 + P],
                         rhs=codes.bitcast(FP8X4),
                         rhs_scale=scales,
@@ -445,11 +445,21 @@ def tile_list_berth_page_nowcast_kernel(
             nc.vector.quantize_mx(out=y_codes[:, cols].bitcast(FP8X4), scales=plane, in_=y_bf[i][:])
             nc.sync.dma_start(y_words[:, cols], y_codes[:, cols].bitcast(I32))
 
-        finish_z(0)
-        w2_codes = sb("w2_codes", PASSES * N, U32, tag="h_last")
+        w2_codes = {}
         w2_sc = sb("w2_sc", PASSES * N, U8)
-        nc.vector.quantize_mx(out=w2_codes[:].bitcast(FP8X4), scales=w2_sc[:], in_=w2_bf[:])
+
+        def quantise_w2(b, tag):
+            w2_codes[b] = sb("w2_codes%d" % b, N, U32, tag=tag)
+            nc.vector.quantize_mx(
+                out=w2_codes[b][:].bitcast(FP8X4),
+                scales=w2_sc[:, b * N : (b + 1) * N],
+                in_=w2_bf[:, b * PACK * N : (b + 1) * PACK * N],
+            )
+
+        quantise_w2(0, "page2")
+        finish_z(0)
         finish_z(1)
+        quantise_w2(1, "strip0")
         quantise_z(0)
         finish_z(2)
         finish_z(3)

@@ -35,6 +35,7 @@ ROUND_RUNS = 64
 STORE_COLUMNS = 1024
 VECTOR_WEIGHS = 5
 TABLE_AHEAD = 1024
+WARM_UPS = 4
 FEATURE_BANKS = [0, 1]
 PAIR_BANKS = [[2, 3, 4, 5, 6, 7], [2, 3, 4, 5, 6, 7, 0, 1], [5, 6, 7, 0]]
 BACK_BANKS = [2, 3, 4]
@@ -457,6 +458,17 @@ def tile_list_berth_page_nowcast_kernel(
             )
 
         quantise_w2(0, "page2")
+        unread = bank(LOW_BANKS[-1], "unread")
+        for i in range(WARM_UPS):
+            nc.tensor.matmul_mx(
+                out=unread[:],
+                lhsT=w2_codes[0][:, :P].bitcast(FP8X4),
+                lhsT_scale=w2_sc[:, :P],
+                rhs=w2_codes[0][:].bitcast(FP8X4),
+                rhs_scale=w2_sc[:, :N],
+                start=True,
+                stop=True,
+            )
         finish_z(0)
         finish_z(1)
         quantise_w2(1, "strip0")

from contextlib import ExitStack

import concourse.mybir as mybir
from concourse.masks import make_identity

K, T, S, T2, H, N = 1024, 4096, 1024, 2048, 1024, 512
FLOPS = 2 * K * H * S + 2 * H * N * T2

F32 = mybir.dt.float32
BF16 = mybir.dt.bfloat16
I32 = mybir.dt.int32
U32 = mybir.dt.uint32
U16 = mybir.dt.uint16
U8 = mybir.dt.uint8
FP8X4 = mybir.dt.float8_e4m3fn_x4
FP4X4 = mybir.dt.float4_e2m1fn_x4
ACT = mybir.ActivationFunctionType
ALU = mybir.AluOpType

P = 128
PACK = 4
BANK = 512
PASSES = 2
TILES = H // P
PAGES = 4
BLOCKS = T2 // P
CHUNKS = T2 // BANK
GROUP = 16
QUADS = 4
ALIGN = 64
FIRST_PIECES = [(0, 128), (128, 256, 512), (512, 1024)]
LAST_GATHERS = [(0, 256), (256, 512), (512, 1024)]
PARTS = [(0, 512, (1, 3)), (512, 512, (1, 3)), (1024, 512, (1, 3)), (1536, 256, ()), (1792, 256, ())]
ROUND_RUNS = 64
STORE_COLUMNS = 1024
VECTOR_WEIGHS = 5
TABLE_AHEAD = 1024
WARM_UPS = 4
FEATURE_BANKS = [0, 1]
PAIR_BANKS = [[2, 3, 4, 5, 6, 7], [2, 3, 4, 5, 6, 7, 0, 1], [5, 6, 7, 0]]
BACK_BANKS = [2, 3, 4]
LOW_BANKS = [1, 2, 3, 4]
LAST_PAIR_BANKS = PAIR_BANKS[2]


def tile_list_berth_page_nowcast_kernel(
    tc, tab_words, tab_scales, offs, w1_words, w1_scales, offs2, wgs, rate, kept, w2, floor, out_0, out_1, out_2
):
    nc = tc.nc
    with ExitStack() as ctx:
        held = ctx.enter_context(tc.tile_pool(name="held", bufs=1))
        shared = ctx.enter_context(tc.tile_pool(name="shared", bufs=1))
        psum = ctx.enter_context(tc.psum_pool(name="psum", bufs=1))

        def sb(name, cols, dtype, tag=None, bufs=1):
            if tag is None:
                return held.tile([P, cols], dtype, name=name, align_bytes=ALIGN)
            return shared.tile([P, cols], dtype, name=name, tag=tag, bufs=bufs, align_bytes=ALIGN)

        def bank(i, name):
            return psum.tile([P, BANK], F32, name=name, tag="bank%d" % i)

        list1 = held.tile([P, S // GROUP], U16, name="list1")
        list2 = held.tile([P, S // GROUP], U16, name="list2")
        rate_sb = sb("rate_sb", TILES, F32)
        floor_sb = sb("floor_sb", PACK, F32)
        one = sb("one", 1, F32)
        unit = sb("unit", 1, F32)
        ident = sb("ident", P, F32)
        tab_sc = sb("tab_sc", T, U8, tag="page3")
        wgs_sb = sb("wgs_sb", S, F32, tag="big2")
        w1_raw = sb("w1_raw", PASSES * 2 * H, U8, tag="zt0")
        w1_sc_raw = sb("w1_sc_raw", H, U8, tag="page2")
        planes1 = [sb("planes1_%d" % a, S + H, U8) for a in range(PASSES)]

        nc.gpsimd.memset(tab_sc[:].bitcast(I32), 0)
        nc.vector.memset(w1_sc_raw[:].bitcast(I32), 0)
        nc.vector.memset(one[:], 1.0)

        nc.gpsimd.memset(planes1[1][:].bitcast(I32), 0)

        nc.scalar.dma_start(
            rate_sb[:].rearrange("p (b t) -> p b t", b=PASSES), rate.rearrange("(b p t) -> p b t", b=PASSES, t=PACK)
        )
        nc.sync.dma_start(
            w1_raw[:].bitcast(I32).rearrange("p (a c) -> p a c", a=PASSES),
            w1_words.bitcast(I32).rearrange("a p c -> p a c"),
        )
        nc.sync.dma_start(list1[:], offs)
        nc.sync.dma_start(wgs_sb[:], wgs)
        tab = [sb("tab%d" % a, T, I32, tag="big%d" % a) for a in range(PASSES)]

        def load_table(a, lo, hi):
            nc.sync.dma_start(tab[a][:, lo:hi], tab_words[a].rearrange("p c i -> p (c i)").bitcast(I32)[:, lo:hi])

        load_table(0, 0, TABLE_AHEAD)
        nc.sync.dma_start(list2[:], offs2)
        for rows, scales in [(tab_sc, tab_scales), (w1_sc_raw, w1_scales)]:
            for a in range(PASSES):
                nc.sync.dma_start(rows[4 * a : P : 8, :].bitcast(I32), scales[a].bitcast(I32))
        load_table(0, TABLE_AHEAD, T)
        load_table(1, 0, T)

        staged = planes1[0]
        v_rows = sb("v_rows", S, U8, tag="page1")
        nc.vector.tensor_copy(v_rows[:], tab_sc[:].indirect(list1[:]))
        nc.vector.tensor_copy(
            staged[:, S:].rearrange("p (b t m) -> p b t m", t=PACK, m=P),
            w1_sc_raw[:].rearrange("p (b m t) -> p b t m", t=PACK, m=P),
        )
        nc.vector.tensor_copy(staged[:, :S].bitcast(I32), v_rows[:].bitcast(I32))
        for a in range(PASSES):
            for i in range(1 - a, 4):
                nc.scalar.dma_start(planes1[a][i:P:32, :].bitcast(I32), staged[8 * i + 4 * a : P : 32, :].bitcast(I32))

        pages = [sb("page0", T2, F32, tag="page0")]
        nc.vector.memset(pages[0][:], 0.0)

        make_identity(nc, ident[:])
        nc.scalar.activation(unit[:], one[:], ACT.Sqrt)

        w1_codes = sb("w1_codes", PASSES * 2 * H, U8, tag="weights")
        nc.scalar.copy(
            w1_codes[:].bitcast(U16).rearrange("p (g t m) -> p g t m", t=PACK, m=P),
            w1_raw[:].bitcast(U16).rearrange("p (g m t) -> p g t m", t=PACK, m=P),
        )

        pages.append(sb("page1", T2, F32, tag="page1"))
        nc.gpsimd.memset(pages[1][:], 0.0)

        v_codes = []

        def gather_words(a, spans):
            halves = [sb("v_codes%d_%d" % (a, i), BANK, U32, tag="strip%d" % (2 * a + i)) for i in range(S // BANK)]
            for lo, hi in spans:
                offsets = list1[:, lo // GROUP : hi // GROUP]
                c0 = lo % BANK
                nc.vector.tensor_copy(halves[lo // BANK][:, c0 : c0 + hi - lo], tab[a][:].bitcast(U32).indirect(offsets))
            v_codes.append(halves)

        gather_words(0, [(0, BANK), (BANK, S)])
        gather_words(1, LAST_GATHERS)

        rw = [sb("rw%d" % i, 2 * S, F32, tag="rw", bufs=4) for i in range(TILES // 2)]

        def weigh(k):
            rw_k = rw[k // 2][:, (k % 2) * S : (k % 2 + 1) * S]
            if k < VECTOR_WEIGHS:
                nc.vector.tensor_scalar_mul(rw_k, wgs_sb[:], rate_sb[:, k : k + 1])
            else:
                nc.scalar.activation(rw_k, wgs_sb[:], ACT.Copy, scale=rate_sb[:, k : k + 1])

        kept_rows = kept.rearrange("(b p u e) m -> b u p e m", b=PASSES, u=2, e=2)
        kept_sb = {}

        def load_kept(pair, rows):
            kept_sb[pair] = sb("kept%d" % pair, rows * T2, F32, tag="big%d" % (2 * (pair % 2)))
            nc.sync.dma_start(
                kept_sb[pair][:].rearrange("p (e m) -> p e m", e=rows), kept_rows[pair // 2, pair % 2][:, :rows, :]
            )

        h = {}

        def product(k, acc, lo, hi, at):
            for a in range(PASSES):
                c0 = a * H + k * P
                nc.tensor.matmul_mx(
                    out=acc[:, at : at + hi - lo],
                    lhsT=w1_codes[:, 2 * c0 : 2 * (c0 + P)].bitcast(FP4X4),
                    lhsT_scale=planes1[a][:, S + k * P : S + (k + 1) * P],
                    rhs=v_codes[a][lo // BANK][:, lo % BANK : lo % BANK + hi - lo].bitcast(FP8X4),
                    rhs_scale=planes1[a][:, lo:hi],
                    start=(a == 0),
                    stop=(a == PASSES - 1),
                )

        def h_tile(k):
            h[k] = sb("h%d" % k, S, F32, tag="h_last") if k == TILES - 1 else sb("h%d" % k, S, F32, tag="h", bufs=TILES - 1)

        def features(k, banks):
            h_tile(k)
            spans = [(0, BANK), (BANK, S)]
            for i, (lo, hi) in enumerate(spans):
                acc = bank(banks[i], "a%d_%d" % (k, i))
                product(k, acc, lo, hi, 0)
                nc.scalar.activation(h[k][:, lo:hi], acc[:], ACT.Square)
            for lo, hi in spans:
                nc.scalar.activation(h[k][:, lo:hi], h[k][:, lo:hi], ACT.Sqrt, bias=unit[:])

        def scatter(k, lo=0, hi=S):
            c0 = (k % 2) * S
            nc.vector.tensor_tensor(
                pages[k % PAGES][:].indirect(list2[:, lo // GROUP : hi // GROUP]),
                h[k][:, lo:hi],
                rw[k // 2][:, c0 + lo : c0 + hi],
                ALU.mult,
            )

        def first_pair():
            for k in range(2):
                h_tile(k)
            for i, runs in enumerate(FIRST_PIECES):
                lo, hi = runs[0], runs[-1]
                for k in range(2):
                    acc = bank((2 * i + k) % 4, "a%d_%d" % (k, i))
                    for n0, n1 in zip(runs, runs[1:]):
                        product(k, acc, n0, n1, n0 - lo)
                    sq = sb("sq%d_%d" % (k, i), hi - lo, F32, tag="page%d" % (k + 2))
                    nc.scalar.activation(sq[:], acc[:, : hi - lo], ACT.Square)
                    nc.scalar.activation(h[k][:, lo:hi], sq[:], ACT.Sqrt, bias=unit[:])
                    scatter(k, lo, hi)
            for i in (2, 3):
                pages.append(sb("page%d" % i, T2, F32, tag="page%d" % i))
                nc.gpsimd.memset(pages[i][:], 0.0)

        sums = {}

        def add_on(pair, g, source, e, first=False, last=False):
            for cc in range(2):
                s0, c0 = (cc * 2 + e) * P, (2 * g + cc) * P
                nc.tensor.matmul(
                    sums[pair, g][:, s0 : s0 + P],
                    source[:, c0 : c0 + P],
                    ident[:],
                    start=first and cc == 0,
                    stop=last and cc == 1,
                    is_transpose=True,
                )

        def add_kept(pair, groups):
            for g in groups:
                banks = PAIR_BANKS[pair]
                sums[pair, g] = bank(banks[g % len(banks)], "sum%d_%d" % (pair, g))
                add_on(pair, g, kept_sb[pair][:, :T2], 0, first=True)
                if pair < 2:
                    add_on(pair, g, kept_sb[pair][:, T2:], 1)

        def add_even(pair, groups):
            for g in groups:
                add_on(pair, g, pages[2 * pair % PAGES], 0)

        def close_pair(pair, zt):
            ahead = len(PAIR_BANKS[pair])
            for g in range(BLOCKS // 2):
                if pair == 2:
                    add_on(pair, g, kept_sb[pair][:, T2:], 1)
                add_on(pair, g, pages[(2 * pair + 1) % PAGES], 1, last=True)
                nc.scalar.copy(
                    zt[:, g * 4 * P : (g + 1) * 4 * P].rearrange("m (c p e) -> m c p e", c=2, e=2),
                    sums[pair, g][:].rearrange("m (c e p) -> m c p e", c=2, e=2),
                )
                again = g - 2 + ahead
                if ahead <= again < BLOCKS // 2:
                    add_kept(pair, [again])
                    add_even(pair, [again])

        low = []

        def add_low(source, first):
            for i, c0 in enumerate(range(0, BLOCKS, 4)):
                if first:
                    low.append(bank(LOW_BANKS[i], "low%d" % i))
                for cc in range(4):
                    nc.tensor.matmul(
                        low[i][:, cc * P : (cc + 1) * P],
                        source[:, (c0 + cc) * P : (c0 + cc + 1) * P],
                        ident[:],
                        start=first and cc == 0,
                        stop=not first and cc == 3,
                        is_transpose=True,
                    )
                if not first:
                    halves = zt[1][:, c0 * 2 * P : (c0 + 4) * 2 * P].rearrange("m (x e) -> m x e", e=2)
                    nc.scalar.copy(halves[:, :, 0], low[i][:])

        def words(zt, c):
            return zt[:, c * 2 * P : (c + 1) * 2 * P].bitcast(F32)

        def back_both(zts, dst, groups):
            for c0 in [2 * g for g in groups]:
                moved = bank(BACK_BANKS[c0 // 2 % len(BACK_BANKS)], "back%d" % c0)
                for u in range(2):
                    for cc in range(2):
                        s0 = (u * 2 + cc) * P
                        nc.tensor.transpose(moved[:, s0 : s0 + P], words(zts[u], c0 + cc), ident[:])
                nc.scalar.copy(
                    dst[:, c0 * PACK * P : (c0 + 2) * PACK * P].bitcast(F32).rearrange("p (m u) -> p m u", u=2),
                    moved[:].rearrange("p (u m) -> p m u", u=2),
                )

        def back_one(zt, dst, u):
            for c0 in range(0, BLOCKS, 4):
                moved = bank(LAST_PAIR_BANKS[c0 // 4], "back_one%d_%d" % (u, c0))
                for cc in range(4):
                    nc.tensor.transpose(moved[:, cc * P : (cc + 1) * P], words(zt, c0 + cc), ident[:])
                w0 = u * T2 + c0 * P
                nc.scalar.copy(dst[:, 2 * w0 : 2 * (w0 + BANK)].bitcast(F32), moved[:])

        load_kept(0, 2)
        load_kept(1, 2)
        w2_raw = sb("w2_raw", PASSES * PACK * N, F32, tag="big1")
        nc.sync.dma_start(
            w2_raw[:].rearrange("p (b x) -> p b x", b=PASSES),
            w2.rearrange("(b p j) n -> p b (j n)", b=PASSES, j=PACK),
        )
        nc.sync.dma_start(floor_sb[:], floor.rearrange("(p t) -> p t", t=PACK))

        for k in range(VECTOR_WEIGHS):
            weigh(k)
        for k in range(VECTOR_WEIGHS, TILES):
            weigh(k)
        first_pair()
        zt = [sb("zt%d" % u, BLOCKS * 2 * P, BF16, tag="zt%d" % u) for u in range(2)]
        z0 = sb("z0", PACK * T2, BF16)
        z1_words = sb("z1_words", PACK * T2, BF16)

        features(2, FEATURE_BANKS)
        scatter(2)
        features(3, FEATURE_BANKS)
        add_kept(0, range(3))
        scatter(3)
        features(4, FEATURE_BANKS)
        add_kept(0, range(3, 6))
        features(5, FEATURE_BANKS)
        add_even(0, range(6))
        features(6, FEATURE_BANKS)
        close_pair(0, zt[0])
        load_kept(2, 2)
        features(7, FEATURE_BANKS)

        w2_bf = sb("w2_bf", PASSES * PACK * N, BF16, tag="weights")
        for b in range(PASSES):
            cols = slice(b * PACK * N, (b + 1) * PACK * N)
            nc.scalar.copy(
                w2_bf[:, cols].rearrange("p (t m j) -> p m j t", t=PACK, j=PACK),
                w2_raw[:, cols].rearrange("p (j m t) -> p m j t", t=PACK, j=PACK),
            )
        last = TILES - 1
        kept_last = []
        for j in range(CHUNKS):
            kept_last.append(sb("kept_last%d" % j, BANK, F32, tag="strip%d" % j))
            nc.sync.dma_start(kept_last[j][:], kept_rows[1, 1][:, 1, j * BANK : (j + 1) * BANK])
        add_kept(1, range(8))
        load_kept(3, 1)
        add_even(1, range(8))
        close_pair(1, zt[1])
        scatter(4)
        scatter(5)
        back_both(zt, z0, range(3))
        add_kept(2, range(4))
        back_both(zt, z0, range(3, 8))
        add_even(2, range(4))
        add_low(kept_sb[3], True)
        close_pair(2, zt[0])
        back_one(zt[0], z1_words, 0)
        scatter(6)
        add_low(pages[2], False)
        back_one(zt[1], z1_words, 1)
        scatter(7)

        z0_sc = sb("z0_sc", T2, U8)
        z1_codes = sb("z1_codes", T2, U32, tag="page0")
        z1_sc = sb("z1_sc", T2, U8)
        y_codes = sb("y_codes", T2, U32)
        y_sc = sb("y_sc", BANK, U8)
        y_rows = out_0.rearrange("(p t) m -> p t m", t=PACK)
        y_words = out_1[0].rearrange("p m t -> p (m t)").bitcast(I32)
        z0_codes, z1, y, y_bf = {}, {}, {}, {}

        def span(j):
            return slice(j * BANK, (j + 1) * BANK)

        def finish_z(j):
            w0 = T2 + j * BANK
            nc.vector.tensor_tensor(
                z1_words[:, 2 * w0 : 2 * (w0 + BANK)].rearrange("p (m e) -> p m e", e=2)[:, :, 1],
                pages[last % PAGES][:, span(j)],
                kept_last[j][:],
                ALU.add,
            )
            z1[j] = sb("z1_%d" % j, PACK * BANK, BF16, tag="h", bufs=TILES - 1)
            nc.scalar.copy(
                z1[j][:].bitcast(F32).rearrange("p (m u) -> p m u", u=2),
                z1_words[:].bitcast(F32).rearrange("p (u m) -> p m u", u=2)[:, span(j), :],
            )

        def quantise_z(j):
            z0_codes[j] = sb("z0_codes%d" % j, BANK, U32, tag="strip%d" % (j + 1) if j + 1 < CHUNKS else "page3")
            nc.vector.quantize_mx(
                out=z0_codes[j][:].bitcast(FP8X4),
                scales=z0_sc[:, span(j)],
                in_=z0[:, PACK * j * BANK : PACK * (j + 1) * BANK],
            )
            nc.vector.quantize_mx(out=z1_codes[:, span(j)].bitcast(FP8X4), scales=z1_sc[:, span(j)], in_=z1[j][:])

        def scores(i):
            lo, width, by_scalar = PARTS[i]
            j, cols = lo // BANK, slice(lo, lo + width)
            y[i] = sb("y%d" % i, PACK * width, F32, tag="rw", bufs=4)
            acc = [bank(PACK * (i % 2) + t, "y%d_%d" % (i, t)) for t in range(PACK)]
            moving = [
                (z0_codes[j][:, lo % BANK : lo % BANK + width], z0_sc[:, cols]),
                (z1_codes[:, cols], z1_sc[:, cols]),
            ]
            for b, (codes, scales) in enumerate(moving):
                for t in range(PACK):
                    c0 = b * N + t * P
                    nc.tensor.matmul_mx(
                        out=acc[t][:, :width],
                        lhsT=w2_codes[b][:, t * P : (t + 1) * P].bitcast(FP8X4),
                        lhsT_scale=w2_sc[:, c0 : c0 + P],
                        rhs=codes.bitcast(FP8X4),
                        rhs_scale=scales,
                        start=(b == 0),
                        stop=(b == PASSES - 1),
                    )
            rows = STORE_COLUMNS // width
            for t in range(PACK):
                y_t = y[i][:, t * width : (t + 1) * width]
                if t in by_scalar:
                    nc.scalar.copy(y_t, acc[t][:, :width])
                    nc.vector.tensor_scalar_max(y_t, y_t, floor_sb[:, t : t + 1])
                else:
                    nc.vector.tensor_scalar_max(y_t, acc[t][:, :width], floor_sb[:, t : t + 1])
                if (t + 1) % rows == 0:
                    nc.sync.dma_start(
                        y_rows[:, t + 1 - rows : t + 1, cols],
                        y[i][:, (t + 1 - rows) * width : (t + 1) * width].rearrange("p (t m) -> p t m", t=rows),
                    )

        def round_y(i):
            width = PARTS[i][1]
            y_bf[i] = sb("y_bf%d" % i, PACK * width, BF16, tag="h", bufs=TILES - 1)
            rounded = y_bf[i][:].rearrange("p (c i t) -> p c t i", t=PACK, i=4)
            by_column = y[i][:].rearrange("p (t c i) -> p c t i", t=PACK, i=4)
            if i == len(PARTS) - 1:
                nc.vector.tensor_copy(rounded, by_column)
            else:
                for c0 in range(0, width // 4, ROUND_RUNS):
                    nc.scalar.copy(rounded[:, c0 : c0 + ROUND_RUNS], by_column[:, c0 : c0 + ROUND_RUNS])

        def planes(i):
            lo, width, by_scalar = PARTS[i]
            cols = slice(lo, lo + width)
            plane = y_sc[4 * (lo // BANK) :, lo % BANK : lo % BANK + width]
            nc.vector.quantize_mx(out=y_codes[:, cols].bitcast(FP8X4), scales=plane, in_=y_bf[i][:])
            nc.sync.dma_start(y_words[:, cols], y_codes[:, cols].bitcast(I32))

        w2_codes = {}
        w2_sc = sb("w2_sc", PASSES * N, U8)

        def quantise_w2(b, tag):
            w2_codes[b] = sb("w2_codes%d" % b, N, U32, tag=tag)
            nc.vector.quantize_mx(
                out=w2_codes[b][:].bitcast(FP8X4),
                scales=w2_sc[:, b * N : (b + 1) * N],
                in_=w2_bf[:, b * PACK * N : (b + 1) * PACK * N],
            )

        quantise_w2(0, "page2")
        unread = bank(LOW_BANKS[-1], "unread")
        for i in range(WARM_UPS):
            nc.tensor.matmul_mx(
                out=unread[:],
                lhsT=w2_codes[0][:, :P].bitcast(FP8X4),
                lhsT_scale=w2_sc[:, :P],
                rhs=w2_codes[0][:].bitcast(FP8X4),
                rhs_scale=w2_sc[:, :N],
                start=True,
                stop=True,
            )
        finish_z(0)
        finish_z(1)
        quantise_w2(1, "strip0")
        quantise_z(0)
        finish_z(2)
        finish_z(3)
        quantise_z(1)
        scores(0)
        quantise_z(2)
        scores(1)
        round_y(0)
        quantise_z(3)
        for i in range(2, len(PARTS)):
            scores(i)
            planes(i - 2)
            round_y(i - 1)
        round_y(len(PARTS) - 1)
        planes(len(PARTS) - 2)
        planes(len(PARTS) - 1)
        for q in range(QUADS):
            queue = nc.sync if q % 2 == 0 else nc.scalar
            rows = out_2[0, 4 * q : 4 * q + 4, :].bitcast(I32).rearrange("r (j c) -> j r c", j=CHUNKS)
            queue.dma_start(rows, y_sc[32 * q : 32 * q + 16, :].bitcast(I32))
